import numpy as np, ml_dtypes
CORES = [16,23,24,31,64,71]
N = 6
import mx_ref
NC = 128
A = np.float32(0.0125)
BF = ml_dtypes.bfloat16
def cut(t, i, w=512):
    return t[:, w * i:w * i + w]
def tile(rs):
    return np.stack(rs, axis=2).reshape(128, -1).astype(BF)
def setup_inputs(rng):
    def f(*shape):
        return mx_ref.flush((rng.standard_normal(shape, dtype=np.float32) * np.exp2(rng.integers(-2, 3, shape[:-1] + (1,)))).astype(BF))
    return {"q": f(N, 128, 4 * NC), "k": f(N, 128, 4 * 512), "v": f(N, 128, 512)}
def setup_inputs_blocks(rng):
    d = setup_inputs(rng)
    for k in ("v",): d[k] = mx_ref.spread(d[k], rng, 4)
    for k in ("q", "k"): d[k] = mx_ref.spread(d[k], rng, 1)
    return d
def setup_inputs_wide(rng):
    d = setup_inputs(rng)
    for k in ("v",): d[k] = mx_ref.flush((d[k].astype(np.float32) * np.exp2(rng.integers(-8, 9, (N, 1, 1))).astype(np.float32)).astype(BF))
    return d
def setup_inputs_sharp(rng):
    d = setup_inputs(rng); v = d["q"].astype(np.float32).reshape(N, 128, -1, 4)
    d["q"] = mx_ref.flush((v * np.exp2(rng.integers(-2, 4, (N, 1, v.shape[2], 1))).astype(np.float32)).reshape(d["q"].shape).astype(BF))
    return d
def setup_inputs_far(rng):
    d = setup_inputs(rng); d["q"] = (d["q"].astype(np.float32) * 10).astype(BF)
    return d
def setup_inputs_faroff(rng):
    d = setup_inputs(rng); v = d["k"].astype(np.float32).reshape(N, 128, -1, 4)
    d["k"] = mx_ref.flush((v + 192 * rng.standard_normal((1, 128, 1, 4), dtype=np.float32)).reshape(d["k"].shape).astype(BF))
    return d
def reference(q, k, v, own=None):
    ONE = mx_ref.quantize(np.ones((128, 512), BF))
    K = [[mx_ref.quantize(cut(k[j], b)) for b in range(4)] for j in range(N)]; V = [mx_ref.quantize(v[j]) for j in range(N)]
    Q = [mx_ref.quantize(q[i]) for i in range(N)]
    lo = np.zeros((N, N, NC), np.float32); w = lo.copy(); wlo = lo.copy(); whi = lo.copy(); p = np.zeros((N, N, 128, 4 * NC), BF); o = np.zeros((N, 128, NC), np.float32)
    S = [[[mx_ref.matmul(K[j][b], Q[i]) * A for b in range(4)] for i in range(N)] for j in range(N)]
    for j in range(N):
        lo[j] = [np.max(s, axis=(0, 1)) for s in S[j]]
    hi = np.broadcast_to(lo.max(axis=0) + 8, lo.shape).copy()
    c = lo if own is None else own["c"]
    for j in range(N):
        for i in range(N):
            p[j][i] = tile([np.exp(np.maximum(s - c[j][i], -20).astype(np.float64)).astype(np.float32) for s in S[j][i]])
    use = p if own is None else own["p"]
    for i in range(N):
        e = np.exp((c[:, i] - c[:, i].max(axis=0)).astype(np.float64)); wlo[i] = e * (1 - 4e-5); whi[i] = e * (1 + 4e-5)
        w[i] = e if own is None else own["w"][i]
        num = den = 0
        for j in range(N):
            P = mx_ref.quantize(use[j][i])
            num = num + w[i][j].astype(np.float64) * mx_ref.matmul(V[j], P); den = den + w[i][j].astype(np.float64) * mx_ref.matmul(ONE, P)
        o[i] = (num / den).astype(np.float32)
    return {"c": c, "c__lo": lo, "c__hi": hi, "p": p, "w": w, "w__lo": wlo, "w__hi": whi, "o": o}

@@ -1,0 +1,453 @@
+import numpy as np
+from concourse.bass import DstId, RemoteDMATransfer
+from concourse.mybir import dt, AluOpType, AxisListType, ActivationFunctionType as AF
+
+NR = 6
+SIM = 80
+A = float(np.float32(0.0125))
+SLACK = 4.0
+LOW = -1e29
+FLOOR = float(np.exp(-20.0))
+RW = 132
+RN = 129
+
+SCRATCH = {
+    "qin": ("sbuf", [128, 512], "bfloat16"), "kin": ("sbuf", [128, 2048], "bfloat16"), "vin": ("sbuf", [128, 512], "bfloat16"),
+    "zer": ("sbuf", [128, 512], "bfloat16"), "one": ("sbuf", [128, 512], "bfloat16"),
+    "qc": ("sbuf", [128, 768], "float8_e4m3fn_x4"), "qs": ("sbuf", [128, 768], "uint8"),
+    "kc": ("sbuf", [128, 512], "float8_e4m3fn_x4"), "ks": ("sbuf", [128, 512], "uint8"),
+    "vc": ("sbuf", [128, 256], "float8_e4m3fn_x4"), "vs": ("sbuf", [128, 256], "uint8"),
+    "pc": ("sbuf", [128, 768], "float8_e4m3fn_x4"), "pp": ("sbuf", [128, 768], "uint8"),
+    "pt": ("sbuf", [128, 3072], "bfloat16"),
+    "s0": ("sbuf", [128, 768], "float32"), "mx": ("sbuf", [128, 768], "float32"), "mb": ("sbuf", [128, 768], "bfloat16"),
+    "mt": ("sbuf", [128, 768], "bfloat16"), "sc": ("sbuf", [128, 768], "bfloat16"), "xh": ("sbuf", [128, 32], "bfloat16"),
+    "d0": ("sbuf", [128, 256], "bfloat16"), "zz": ("sbuf", [128, 768], "bfloat16"), "fi": ("sbuf", [128, 768], "bfloat16"),
+    "cb": ("sbuf", [128, 768], "bfloat16"), "yy": ("sbuf", [128, 3072], "float32"), "rr": ("sbuf", [128, 3072], "float32"),
+    "co": ("sbuf", [128, 32], "float32"), "ct": ("sbuf", [128, 32], "float32"), "cl": ("sbuf", [128, 24], "float32"),
+    "nm": ("sbuf", [128, 4], "float32"), "wt": ("sbuf", [128, 32], "float32"), "wo": ("sbuf", [128, 32], "float32"),
+    "sr": ("sbuf", [128, NR * RW], "float32"), "ar": ("sbuf", [128, NR * RW], "float32"), "uu": ("sbuf", [128, NR * RW], "float32"),
+    "ac": ("sbuf", [128, RW], "float32"), "rc": ("sbuf", [128, 4], "float32"), "on": ("sbuf", [128, 128], "float32"),
+    "ot": ("sbuf", [128, 128], "float32"),
+    "hc": ("sbuf", [128, 128], "float8_e4m3fn_x4"), "hs": ("sbuf", [128, 128], "uint8"),
+    "hl": ("sbuf", [128, 8], "float32"), "ha": ("sbuf", [128, 2 * RW], "float32"),
+    "ps": ("psum", [128, 4096], "float32"),
+}
+SEMAPHORES = (["v", "s", "t", "lq", "lv", "st", "sent", "carr", "hqc", "hqs", "hc0", "hc1", "ha0", "ha1"]
+              + ["lk%d" % b for b in range(4)] + ["q%d" % i for i in range(NR)] + ["a%d" % i for i in range(NR)])
+
+PLACES = ((0,), (1, 2), (3, 4), (5,))
+VCLAMP = (False, False, True, True)
+EARLY = 4
+
+
+def engines(mask, n, k=0):
+    bits = [e for e in range(16) if (mask >> e) & 1][k * n:k * n + n]
+    return sum(1 << e for e in bits)
+
+
+def links(topo, a, b):
+    x, y, d = topo.chip(a), topo.chip(b), topo.die(a)
+    if x == y:
+        return []
+    if topo.mates(x, y):
+        return [("mate", d, x, y)]
+    if topo.same_plane(x, y):
+        return [("out", d, x), ("in", d, y)]
+    m = [z for z in range(topo.chip(SIM - 1) + 1) if topo.mates(x, z)][0]
+    return [("mate", d, x, m), ("out", d, m), ("in", d, y)]
+
+
+def make_plan(T, topo):
+    cores = list(T.cores)
+    load = {}
+    for a in cores:
+        for b in cores:
+            if a != b and topo.may_write(a, b):
+                for l in links(topo, a, b):
+                    load[l] = load.get(l, 0) + 1
+    relay, used = {}, set(cores)
+    for a in cores:
+        barred = [b for b in cores if a != b and not topo.may_write(a, b)]
+        for ch in sorted(set(topo.chip(b) for b in barred)):
+            dsts = [b for b in barred if topo.chip(b) == ch]
+            best = None
+            for h in range(SIM):
+                if h in used or not topo.may_write(a, h) or not all(topo.may_write(h, b) for b in dsts):
+                    continue
+                extra = {}
+                for l in links(topo, a, h) + [l for b in dsts for l in links(topo, h, b)]:
+                    extra[l] = extra.get(l, 0) + 1
+                key = (max(load.get(l, 0) + n for l, n in extra.items()), sum(extra.values()), topo.die(h) != topo.die(a), h)
+                if best is None or key < best[0]:
+                    best = (key, h, extra)
+            used.add(best[1])
+            for l, n in best[2].items():
+                load[l] = load.get(l, 0) + n
+            for b in dsts:
+                relay[(a, b)] = best[1]
+    order = {}
+    for j in cores:
+        mate = [i for i in cores if i != j and topo.chip(i) == topo.chip(j)]
+        rest = [i for i in cores if i != j and i not in mate]
+        rest.sort(key=lambda i: ((i, j) in relay, (j, i) not in relay, i))
+        late = sorted(rest[2:], key=lambda i: ((j, i) not in relay, i))
+        by_place = [j] + rest[:2] + late + mate
+        order[j] = [by_place[p] for ps in PLACES for p in ps]
+    return relay, order
+
+
+def dest(topo, c):
+    a = topo.addr(c)
+    return DstId(rid=a[0], pnc=a[1])
+
+
+def rank_program(g, core, T, topo):
+    relay, order = make_plan(T, topo)
+    cores = list(T.cores)
+    sem = T.sem
+    sent = [0]
+    groups, at = [], 0
+    for ps in PLACES:
+        groups.append(tuple(range(at, at + len(ps))))
+        at += len(ps)
+    group_of = [k for k, s in enumerate(groups) for _ in s]
+    ng = len(groups)
+
+    def send(src, pieces, rsem, n, k=0):
+        m = 0xFFFF
+        for c, _ in pieces:
+            m &= topo.mask(core, c)
+        m = engines(m, n, k)
+        g.remote_dma_fused([RemoteDMATransfer(dst_ids=[dest(topo, c) for c, _ in pieces], dma_engine_mask=m, remote_sem=sem[rsem],
+                                              srcs=[src], dsts=[p for _, p in pieces])], local_sem=sem["sent"])
+        sent[0] += n
+
+    def codes(buf, a, b):
+        return buf[:, a:b].bitcast(dt.uint8)
+
+    def qslot(src, dst):
+        return order[dst].index(src)
+
+    def lane(b, n):
+        return (n, 8 // n) if topo.chip(b) == topo.chip(core) else (n, 0)
+
+    def put_q(src, dsts, cbuf, sbuf, name, n, k=0):
+        to = {b: slice(128 * qslot(src, b), 128 * qslot(src, b) + 128) for b in dsts}
+        send(codes(cbuf, 0, 128), [(b, codes(T.qc, to[b].start, to[b].stop)) for b in dsts], name, n, k)
+        yield
+        send(sbuf[:, 0:128], [(b, T.qs[:, to[b]]) for b in dsts], name, n, k)
+
+    rank = T.rank_of(core)
+    if rank is None:
+        mine = sorted((a, b) for (a, b), h in relay.items() if h == core)
+        if not mine:
+            return
+        src = mine[0][0]
+        sr = T.rank_of(src)
+        dsts = sorted([b for _, b in mine], key=lambda b: order[src].index(b))
+        g.wait_ge(sem["hqc"], 8)
+        for _ in put_q(src, dsts, T.hc, T.hs, "q%d" % sr, 8):
+            g.wait_ge(sem["hqs"], 8)
+        for k, b in enumerate(dsts):
+            g.wait_ge(sem["hc%d" % k], 4)
+            send(T.hl[:, 4 * k:4 * k + 4], [(b, T.cl[:, 4 * sr:4 * sr + 4])], "carr", 4)
+        for k, b in enumerate(dsts):
+            g.wait_ge(sem["ha%d" % k], 8)
+            send(T.ha[:, RW * k:RW * k + RN], [(b, T.ar[:, RW * sr:RW * sr + RN])], "a%d" % sr, 8)
+        g.wait_ge(sem["sent"], sent[0])
+        return
+
+    me = order[core]
+    rk = [T.rank_of(c) for c in me]
+    queue = {"v": g.vector, "s": g.scalar, "t": g.tensor, "g": g, "y": g.sync}
+    count = {"v": 0, "s": 0, "t": 0}
+    seen = {q: {} for q in queue}
+
+    def need(q, deps):
+        want = {}
+        for name, n in deps:
+            want[name] = max(want.get(name, 0), n)
+        for name, n in want.items():
+            if seen[q].get(name, 0) < n:
+                queue[q].wait_ge(sem[name], n)
+                seen[q][name] = n
+
+    def op(q, call, deps):
+        need(q, deps)
+        call(queue[q]).then_inc(sem[q], 1)
+        count[q] += 1
+        return (q, count[q])
+
+    def run(fs):
+        for f in fs:
+            f()
+
+    def bank(k, n):
+        return T.ps[:, 512 * k:512 * k + n]
+
+    add, mul, sub, mxm = AluOpType.add, AluOpType.mult, AluOpType.subtract, AluOpType.max
+
+    g.sync.dma_start(T.qin[:, 0:256], T.q[:, 0:256]).then_inc(sem["lq"], 16)
+    g.scalar.dma_start(T.qin[:, 256:512], T.q[:, 256:512]).then_inc(sem["lq"], 16)
+    for b in range(4):
+        (g.scalar if b % 2 == 0 else g.sync).dma_start(T.kin[:, 512 * b:512 * b + 512], T.k[:, 512 * b:512 * b + 512]).then_inc(sem["lk%d" % b], 16)
+    g.scalar.dma_start(T.vin[:], T.v[:]).then_inc(sem["lv"], 16)
+
+    t_zer = op("v", lambda e: e.memset(T.zer[:], 0.0), [])
+    t_one = op("s", lambda e: e.activation(T.one[:], T.zer[:], AF.Exp), [t_zer])
+    t_d = op("v", lambda e: e.memset(T.d0[:], 0.0), [])
+    t_z = op("v", lambda e: e.memset(T.zz[:], LOW), [])
+    t_d = op("v", lambda e: e.memset(T.d0[:, 0:256:32], LOW), [t_d])
+    t_w = op("v", lambda e: e.memset(T.wt[:], 0.0), [])
+    t_c = op("v", lambda e: e.memset(T.co[:], 0.0), [])
+
+    t_q = op("v", lambda e: e.quantize_mx(T.qc[:, 0:128], T.qs[:, 0:128], T.qin[:]), [("lq", 32)])
+    need("g", [t_q])
+    mate = [b for b in cores if b != core and topo.chip(b) == topo.chip(core)]
+    far = [b for b in cores if b != core and b not in mate]
+    rel = []
+    for b in far:
+        if (core, b) in relay and relay[(core, b)] not in rel:
+            rel.append(relay[(core, b)])
+    far = sorted([b for b in far if (core, b) not in relay], key=lambda b: (group_of[qslot(core, b)], (b, core) not in relay, b))
+    for h in reversed(rel):
+        send(codes(T.qc, 0, 128), [(h, codes(T.hc, 0, 128))], "hqc", *lane(h, 8))
+        send(T.qs[:, 0:128], [(h, T.hs[:, 0:128])], "hqs", *lane(h, 8))
+    for b in mate + far:
+        for _ in put_q(core, [b], T.qc, T.qs, "q%d" % rank, *lane(b, 8)):
+            pass
+    t_V1 = op("v", lambda e: e.quantize_mx(T.vc[:, 128:256], T.vs[:, 128:256], T.one[:]), [t_one])
+    t_k = [op("v", lambda e: e.quantize_mx(T.kc[:, 128 * b:128 * b + 128], T.ks[:, 128 * b:128 * b + 128], T.kin[:, 512 * b:512 * b + 512]),
+              [("lk%d" % b, 16)]) for b in range(4)]
+
+    banks, pvbank = [], []
+    for gi, sl in enumerate(groups):
+        bs = list(range(4 * (gi % 2), 4 * (gi % 2) + 4)) if gi < 2 else banks[gi - 2]
+        if gi >= 2:
+            m = len(groups[gi - 2])
+            bs = bs[m:] + bs[:m]
+        banks.append(bs)
+        pvbank += bs[:len(sl)]
+    free = {k: [] for k in range(8)}
+    tS, tSub, tE, tQ, tPV, tEv, tC, tCo, tK = {}, {}, {}, {}, {}, {}, {}, {}, {}
+
+    def cols(gi):
+        s = groups[gi]
+        return 128 * s[0], 128 * len(s)
+
+    def scores(gi):
+        o, n = cols(gi)
+        deps = [t_q if s == 0 else ("q%d" % rk[s], 16) for s in groups[gi]]
+        for b in range(4):
+            k = banks[gi][b]
+            tS[gi, b] = op("t", lambda e: e.matmul_mx(bank(k, n), T.kc[:, 128 * b:128 * b + 128], T.ks[:, 128 * b:128 * b + 128],
+                                                      T.qc[:, o:o + n], T.qs[:, o:o + n], True, True), deps + [t_k[b]] + free[k])
+
+    def first(gi):
+        o, n = cols(gi)
+        tC[gi] = op("s", lambda e: e.activation(T.s0[:, o:o + n], bank(banks[gi][0], n), AF.Copy), [tS[gi, 0]])
+
+    def shift(gi):
+        o, n = cols(gi)
+        nb = n // 32
+        h = {}
+        ps = [128 * x for x in groups[gi]]
+
+        def mx(p, c):
+            def f():
+                in0 = (T.s0 if c == 1 else T.mx)[:, p:p + 128]
+                k = 512 * banks[gi][c] + p - o
+                h[p] = op("v", lambda e: e.tensor_tensor((T.mb if c == 3 else T.mx)[:, p:p + 128], in0, T.ps[:, k:k + 128], mxm),
+                          [tC[gi] if c == 1 else h[p], tS[gi, c]])
+            return f
+
+        def tr(p):
+            def f():
+                h[p] = op("v", lambda e: e.transpose(T.mt[:, p:p + 128], T.mb[:, p:p + 128]), [h[p]])
+            return f
+
+        def sc(p):
+            def f():
+                h[p] = op("v", lambda e: e.tensor_tensor_scan(T.sc[:, p:p + 128], T.d0[:, 0:128], T.mt[:, p:p + 128], LOW, add, mxm), [h[p], t_d])
+            return f
+
+        def xh():
+            h["x"] = op("v", lambda e: e.tensor_tensor(T.xh[0:64, o // 32:o // 32 + nb], T.sc[0:64, o + 31:o + n:32], T.sc[64:128, o + 31:o + n:32], mxm),
+                        [h[p] for p in ps])
+
+        def vq(a):
+            def f():
+                h["z"] = op("v", lambda e: e.tensor_tensor(T.zz[32 * a:32 * a + 32, o:o + n:32], T.xh[0:32, o // 32:o // 32 + nb],
+                                                           T.xh[32:64, o // 32:o // 32 + nb], mxm), [h["x"], t_z])
+            return f
+
+        def fi(p):
+            def f():
+                h[p] = op("v", lambda e: e.tensor_tensor_scan(T.fi[:, p:p + 128], T.d0[:, 0:128], T.zz[:, p:p + 128], LOW, add, mxm), [h["z"]])
+            return f
+
+        def t2(p):
+            def f():
+                tC[gi, "b"] = op("v", lambda e: e.transpose(T.cb[:, p:p + 128], T.fi[:, p:p + 128]), [h[p]])
+            return f
+
+        def co(x):
+            def f():
+                for out in [T.co[:, 4 * rk[x]:4 * rk[x] + 4]] + ([T.cl[:, 4 * rank:4 * rank + 4]] if x == 0 else []):
+                    tCo[gi] = op("s", lambda e: e.activation(out, T.zz[:, 128 * x:128 * x + 128:32], AF.Copy, bias=SLACK, scale=A), [h["z"], t_c])
+            return f
+
+        return ([mx(p, c) for c in (1, 2, 3) for p in ps] + [tr(p) for p in ps] + [sc(p) for p in ps] + [xh],
+                [vq(a) for a in range(4)], [fi(p) for p in ps], [co(x) for x in groups[gi]], [t2(p) for p in ps])
+
+    pend = []
+
+    def subtract(gi, b):
+        o, n = cols(gi)
+        k = banks[gi][b]
+        y = 4 * o + b * n
+        tSub[gi, b] = op("v", lambda e: e.tensor_tensor(T.yy[:, y:y + n], bank(k, n), T.cb[:, o:o + n], sub), [tC[gi, "b"]])
+        free[k] = [tSub[gi, b]]
+
+    def relu(gi, b):
+        o, n = cols(gi)
+        y = 4 * o + b * n
+        t = None
+        if not VCLAMP[gi]:
+            t = op("s", lambda e: e.activation(T.rr[:, y:y + n], T.yy[:, y:y + n], AF.Relu, bias=20.0 - SLACK, scale=A), [tSub[gi, b]])
+        pend.append((gi, b, t))
+
+    def expo():
+        gi, b, t = pend.pop(0)
+        o, n = cols(gi)
+        y = 4 * o + b * n
+        out = T.pt[:, 4 * o + b:4 * o + 4 * n:4]
+        if t is None:
+            tE[gi] = op("s", lambda e: e.activation(out, T.yy[:, y:y + n], AF.Exp, bias=-SLACK, scale=A), [tSub[gi, b]])
+        else:
+            tE[gi] = op("s", lambda e: e.activation(out, T.rr[:, y:y + n], AF.Exp, bias=-20.0), [t])
+
+    nst = [0]
+
+    def store(out, in_, deps):
+        need("y", deps)
+        g.sync.dma_start(out, in_).then_inc(sem["st"], 16)
+        nst[0] += 16
+
+    def quant(gi):
+        for s in groups[gi]:
+            tK[s] = tE[gi]
+            if VCLAMP[gi]:
+                tK[s] = op("v", lambda e: e.tensor_scalar(T.pt[:, 512 * s:512 * s + 512], T.pt[:, 512 * s:512 * s + 512], FLOOR, None, mxm), [tE[gi]])
+        for s in groups[gi]:
+            tQ[s] = op("v", lambda e: e.quantize_mx(T.pc[:, 128 * s:128 * s + 128], T.pp[:, 128 * s:128 * s + 128], T.pt[:, 512 * s:512 * s + 512]), [tK[s]])
+            store(T.p[rk[s]], T.pt[:, 512 * s:512 * s + 512], [tK[s]])
+
+    def values(gi):
+        for s in groups[gi]:
+            k = pvbank[s]
+            tPV[s] = op("t", lambda e: e.matmul_mx(bank(k, 256), T.pc[:, 128 * s:128 * s + 128], T.pp[:, 128 * s:128 * s + 128],
+                                                   T.vc[:, 0:256], T.vs[:, 0:256], True, True), [tQ[s], t_v, t_V1] + free[k])
+
+    def evac(gi):
+        for s in groups[gi]:
+            tEv[s] = op("s", lambda e: e.activation(T.sr[:, RW * s:RW * s + RN], bank(pvbank[s], RN), AF.Copy), [tPV[s]])
+            free[pvbank[s]] = [tEv[s]]
+
+    def hk(b):
+        h = relay[(core, b)]
+        return h, [x for x in me if relay.get((core, x)) == h].index(b)
+
+    def send_c(gi):
+        need("g", [tCo[gi]])
+        trs, on = [], {}
+        for s in [s for s in groups[gi] if s]:
+            b, to, land, name = me[s], me[s], T.cl[:, 4 * rank:4 * rank + 4], "carr"
+            if (core, b) in relay:
+                to, k = hk(b)
+                land, name = T.hl[:, 4 * k:4 * k + 4], "hc%d" % k
+            n, k = lane(to, 4)
+            on[k] = on.get(k, -1) + 1
+            trs.append(RemoteDMATransfer(dst_ids=[dest(topo, to)], dma_engine_mask=engines(topo.mask(core, to), n, k + on[k]), remote_sem=sem[name],
+                                         srcs=[T.co[:, 4 * rk[s]:4 * rk[s] + 4]], dsts=[land]))
+            sent[0] += n
+        g.remote_dma_fused(trs, local_sem=sem["sent"])
+
+    def send_a(gi):
+        for s in [s for s in groups[gi] if s]:
+            b, src = me[s], T.sr[:, RW * s:RW * s + RN]
+            need("g", [tEv[s]])
+            if (core, b) in relay:
+                h, k = hk(b)
+                send(src, [(h, T.ha[:, RW * k:RW * k + RN])], "ha%d" % k, *lane(h, 8))
+            else:
+                send(src, [(b, T.ar[:, RW * rank:RW * rank + RN])], "a%d" % rank, *lane(b, 8))
+
+    scores(0)
+    first(0)
+    up, vq, fi, co, t2 = shift(0)
+    run(up[:-1])
+    t_v = op("v", lambda e: e.quantize_mx(T.vc[:, 0:128], T.vs[:, 0:128], T.vin[:]), [("lv", 16)])
+    run(up[-1:]), run(vq), run(fi), run(co), run(t2)
+    scores(1)
+    for gi in range(ng):
+        last = gi == ng - 1
+        if not last:
+            up, vq, fi, co, t2 = shift(gi + 1)
+        if gi and not last:
+            evac(gi - 1)
+            send_a(gi - 1)
+            scores(gi + 1)
+        for b in range(4):
+            subtract(gi, b), relu(gi, b)
+            if b:
+                expo()
+            if b == 0 and not last:
+                first(gi + 1)
+        expo()
+        if not last:
+            early = EARLY if gi == ng - 2 else len(up)
+            run(up[:early])
+            if gi == ng - 2:
+                quant(gi), values(gi), evac(gi), send_a(gi)
+            run(up[early:]), run(vq), run(co)
+            send_c(gi + 1)
+            run(fi)
+            if gi < ng - 2:
+                quant(gi), values(gi)
+            run(t2)
+    quant(ng - 1), values(ng - 1), evac(ng - 1), send_a(ng - 1)
+
+    t_ct = op("v", lambda e: e.transpose(T.ct[0:32, :], T.co[0:32, :]), [tCo[gi] for gi in range(ng)])
+    store(T.c[:], T.ct[0:24, :], [t_ct])
+
+    tw = []
+    for b in range(4):
+        tw.append(op("v", lambda e: e.tensor_reduce(T.nm[32 * b:32 * b + 32, 0:1], T.cl[32 * b:32 * b + 32, b:24:4], AxisListType.X, mxm, negate=True),
+                     [("carr", 20), tCo[0]]))
+    tw = [op("s", lambda e: e.activation(T.wt[32 * b:32 * b + 32, 0:6], T.cl[32 * b:32 * b + 32, b:24:4], AF.Exp, bias=T.nm[32 * b:32 * b + 32, 0:1]),
+             [tw[b], t_w, ("carr", 20), tCo[0]]) for b in range(4)]
+    t_wo = op("v", lambda e: e.transpose(T.wo[:], T.wt[:]), tw)
+    for b in range(4):
+        store(T.w[:, 32 * b:32 * b + 32], T.wo[32 * b:32 * b + 6, :], [t_wo])
+
+    def when(j):
+        return group_of[order[j].index(core)] + 1.5 * ((j, core) in relay), j
+
+    acc = None
+    for k, j in enumerate([core] + sorted([j for j in cores if j != core], key=when)):
+        r = T.rank_of(j)
+        src = T.sr[:, 0:RN] if k == 0 else T.ar[:, RW * r:RW * r + RN]
+        out = T.ac[:, 0:RN] if k == 0 else T.uu[:, RW * r:RW * r + RN]
+        t = op("s", lambda e: e.activation(out, src, AF.Copy, scale=T.wt[:, r:r + 1]), tw + ([tEv[0]] if k == 0 else [("a%d" % r, 8)]))
+        acc = t if k == 0 else op("v", lambda e: e.tensor_tensor(T.ac[:, 0:RN], T.ac[:, 0:RN], T.uu[:, RW * r:RW * r + RN], add), [acc, t])
+    t_rc = op("v", lambda e: e.reciprocal(T.rc[:, 0:1], T.ac[:, 128:129]), [acc])
+    t_on = op("v", lambda e: e.tensor_scalar(T.on[:], T.ac[:, 0:128], T.rc[:, 0:1], None, mul), [t_rc])
+    for b in range(4):
+        for a in range(4):
+            t = op("v", lambda e: e.transpose(T.ot[32 * b:32 * b + 32, 32 * a:32 * a + 32], T.on[32 * a:32 * a + 32, 32 * b:32 * b + 32]), [t_on])
+        store(T.o[32 * b:32 * b + 32, :], T.ot[32 * b:32 * b + 32, :], [t])
+
+    g.sync.wait_ge(sem["st"], nst[0])
+    need("g", [(q, count[q]) for q in count])
+    g.wait_ge(sem["sent"], sent[0])

@@ -5,7 +5,6 @@ from concourse.mybir import dt, AluOpType, AxisListType, ActivationFunctionType 
 NR = 6
 SIM = 80
 A = float(np.float32(0.0125))
-SLACK = 4.0
 LOW = -1e29
 FLOOR = float(np.exp(-20.0))
 RW = 132
@@ -19,11 +18,9 @@ SCRATCH = {
     "vc": ("sbuf", [128, 256], "float8_e4m3fn_x4"), "vs": ("sbuf", [128, 256], "uint8"),
     "pc": ("sbuf", [128, 768], "float8_e4m3fn_x4"), "pp": ("sbuf", [128, 768], "uint8"),
     "pt": ("sbuf", [128, 3072], "bfloat16"),
-    "s0": ("sbuf", [128, 768], "float32"), "mx": ("sbuf", [128, 768], "float32"), "mb": ("sbuf", [128, 768], "bfloat16"),
-    "mt": ("sbuf", [128, 768], "bfloat16"), "sc": ("sbuf", [128, 768], "bfloat16"), "xh": ("sbuf", [128, 32], "bfloat16"),
-    "d0": ("sbuf", [128, 256], "bfloat16"), "zz": ("sbuf", [128, 768], "bfloat16"), "fi": ("sbuf", [128, 768], "bfloat16"),
-    "cb": ("sbuf", [128, 768], "bfloat16"), "yy": ("sbuf", [128, 3072], "float32"), "rr": ("sbuf", [128, 3072], "float32"),
-    "co": ("sbuf", [128, 32], "float32"), "ct": ("sbuf", [128, 32], "float32"), "cl": ("sbuf", [128, 24], "float32"),
+    "s0": ("sbuf", [128, 1536], "float32"), "fm": ("sbuf", [128, 1536], "float32"), "nb": ("sbuf", [128, 8], "float32"),
+    "ee": ("sbuf", [128, 24, 128], "bfloat16"), "zz": ("sbuf", [128, 3072], "bfloat16"), "yy": ("sbuf", [128, 3072], "bfloat16"),
+    "cc": ("sbuf", [128, 32], "float32"), "ct": ("sbuf", [128, 32], "float32"), "cl": ("sbuf", [128, 24], "float32"),
     "nm": ("sbuf", [128, 4], "float32"), "wt": ("sbuf", [128, 32], "float32"), "wo": ("sbuf", [128, 32], "float32"),
     "sr": ("sbuf", [128, NR * RW], "float32"), "ar": ("sbuf", [128, NR * RW], "float32"), "uu": ("sbuf", [128, NR * RW], "float32"),
     "ac": ("sbuf", [128, RW], "float32"), "rc": ("sbuf", [128, 4], "float32"), "on": ("sbuf", [128, 128], "float32"),
@@ -32,12 +29,14 @@ SCRATCH = {
     "hl": ("sbuf", [128, 8], "float32"), "ha": ("sbuf", [128, 2 * RW], "float32"),
     "ps": ("psum", [128, 4096], "float32"),
 }
-SEMAPHORES = (["v", "s", "t", "lq", "lv", "st", "sent", "carr", "hqc", "hqs", "hc0", "hc1", "ha0", "ha1"]
+SEMAPHORES = (["v", "s", "t", "lq", "lv", "st", "sent", "carr", "hqc", "hqs", "hc0", "hc1", "ha0", "ha1", "y0", "y2", "y4"]
               + ["lk%d" % b for b in range(4)] + ["q%d" % i for i in range(NR)] + ["a%d" % i for i in range(NR)])
 
-PLACES = ((0,), (1, 2), (3, 4), (5,))
-VCLAMP = (False, False, True, True)
-EARLY = 4
+GROUP = (0, 1, 2, 2, 3, 3)
+DONE = (0, 1.6, 0, 0.7, 2.5, 3.1)
+HOP = 2.0
+PLAN = """S0 h0 m0 V b0 e0 S1 h1 t0 m1 b1 e1 S2 S3 C1 t1 Y0 h2 h3 m2 m3 b2 e2 b3 C23 e3 t2 t3 Y2 S4 S5 h4 h5 m4 m5 b4 e4 b5 C45 e5 t4 t5 Y4
+c2 q2 x2 c3 q3 x3 v23 A23 c10 q10 x10 v10 A1 c4 q4 x4 c5 q5 x5 v45 A45"""
 
 
 def engines(mask, n, k=0):
@@ -85,15 +84,20 @@ def make_plan(T, topo):
                 load[l] = load.get(l, 0) + n
             for b in dsts:
                 relay[(a, b)] = best[1]
+    first, turns = {}, {}
+    for (a, b), h in sorted(relay.items()):
+        both = sorted(y for (x, y), z in relay.items() if (x, z) == (a, h))
+        if (a, h) not in first:
+            first[(a, h)] = min(both, key=lambda y: (turns.get(y, 0), y))
+            turns[first[(a, h)]] = turns.get(first[(a, h)], 0) + 1
     order = {}
     for j in cores:
         mate = [i for i in cores if i != j and topo.chip(i) == topo.chip(j)]
         rest = [i for i in cores if i != j and i not in mate]
         rest.sort(key=lambda i: ((i, j) in relay, (j, i) not in relay, i))
-        late = sorted(rest[2:], key=lambda i: ((j, i) not in relay, i))
-        by_place = [j] + rest[:2] + late + mate
-        order[j] = [by_place[p] for ps in PLACES for p in ps]
-    return relay, order
+        late = sorted(rest[2:], key=lambda i: ((i, j) in relay and first[(i, relay[(i, j)])] != j, i))
+        order[j] = [j] + mate + rest[:2] + late
+    return relay, order, first
 
 
 def dest(topo, c):
@@ -102,16 +106,10 @@ def dest(topo, c):
 
 
 def rank_program(g, core, T, topo):
-    relay, order = make_plan(T, topo)
+    relay, order, first = make_plan(T, topo)
     cores = list(T.cores)
     sem = T.sem
     sent = [0]
-    groups, at = [], 0
-    for ps in PLACES:
-        groups.append(tuple(range(at, at + len(ps))))
-        at += len(ps)
-    group_of = [k for k, s in enumerate(groups) for _ in s]
-    ng = len(groups)
 
     def send(src, pieces, rsem, n, k=0):
         m = 0xFFFF
@@ -146,11 +144,13 @@ def rank_program(g, core, T, topo):
         sr = T.rank_of(src)
         dsts = sorted([b for _, b in mine], key=lambda b: order[src].index(b))
         g.wait_ge(sem["hqc"], 8)
-        for _ in put_q(src, dsts, T.hc, T.hs, "q%d" % sr, 8):
-            g.wait_ge(sem["hqs"], 8)
+        for n, b in enumerate(sorted(dsts, key=lambda b: (b != first[(src, core)], b))):
+            for _ in put_q(src, [b], T.hc, T.hs, "q%d" % sr, 8):
+                if n == 0:
+                    g.wait_ge(sem["hqs"], 8)
         for k, b in enumerate(dsts):
             g.wait_ge(sem["hc%d" % k], 4)
-            send(T.hl[:, 4 * k:4 * k + 4], [(b, T.cl[:, 4 * sr:4 * sr + 4])], "carr", 4)
+            send(T.hl[:, 4 * k:4 * k + 1], [(b, T.cl[:, 4 * sr:4 * sr + 1])], "carr", 4)
         for k, b in enumerate(dsts):
             g.wait_ge(sem["ha%d" % k], 8)
             send(T.ha[:, RW * k:RW * k + RN], [(b, T.ar[:, RW * sr:RW * sr + RN])], "a%d" % sr, 8)
@@ -178,14 +178,10 @@ def rank_program(g, core, T, topo):
         count[q] += 1
         return (q, count[q])
 
-    def run(fs):
-        for f in fs:
-            f()
+    def bank(k, a, b):
+        return T.ps[:, 512 * k + a:512 * k + b]
 
-    def bank(k, n):
-        return T.ps[:, 512 * k:512 * k + n]
-
-    add, mul, sub, mxm = AluOpType.add, AluOpType.mult, AluOpType.subtract, AluOpType.max
+    add, mul, mxm = AluOpType.add, AluOpType.mult, AluOpType.max
 
     g.sync.dma_start(T.qin[:, 0:256], T.q[:, 0:256]).then_inc(sem["lq"], 16)
     g.scalar.dma_start(T.qin[:, 256:512], T.q[:, 256:512]).then_inc(sem["lq"], 16)
@@ -195,11 +191,8 @@ def rank_program(g, core, T, topo):
 
     t_zer = op("v", lambda e: e.memset(T.zer[:], 0.0), [])
     t_one = op("s", lambda e: e.activation(T.one[:], T.zer[:], AF.Exp), [t_zer])
-    t_d = op("v", lambda e: e.memset(T.d0[:], 0.0), [])
-    t_z = op("v", lambda e: e.memset(T.zz[:], LOW), [])
-    t_d = op("v", lambda e: e.memset(T.d0[:, 0:256:32], LOW), [t_d])
     t_w = op("v", lambda e: e.memset(T.wt[:], 0.0), [])
-    t_c = op("v", lambda e: e.memset(T.co[:], 0.0), [])
+    t_c = op("v", lambda e: e.memset(T.cc[:], 0.0), [])
 
     t_q = op("v", lambda e: e.quantize_mx(T.qc[:, 0:128], T.qs[:, 0:128], T.qin[:]), [("lq", 32)])
     need("g", [t_q])
@@ -209,7 +202,7 @@ def rank_program(g, core, T, topo):
     for b in far:
         if (core, b) in relay and relay[(core, b)] not in rel:
             rel.append(relay[(core, b)])
-    far = sorted([b for b in far if (core, b) not in relay], key=lambda b: (group_of[qslot(core, b)], (b, core) not in relay, b))
+    far = sorted([b for b in far if (core, b) not in relay], key=lambda b: (GROUP[qslot(core, b)], (b, core) not in relay, b))
     for h in reversed(rel):
         send(codes(T.qc, 0, 128), [(h, codes(T.hc, 0, 128))], "hqc", *lane(h, 8))
         send(T.qs[:, 0:128], [(h, T.hs[:, 0:128])], "hqs", *lane(h, 8))
@@ -219,235 +212,146 @@ def rank_program(g, core, T, topo):
     t_V1 = op("v", lambda e: e.quantize_mx(T.vc[:, 128:256], T.vs[:, 128:256], T.one[:]), [t_one])
     t_k = [op("v", lambda e: e.quantize_mx(T.kc[:, 128 * b:128 * b + 128], T.ks[:, 128 * b:128 * b + 128], T.kin[:, 512 * b:512 * b + 512]),
               [("lk%d" % b, 16)]) for b in range(4)]
-
-    banks, pvbank = [], []
-    for gi, sl in enumerate(groups):
-        bs = list(range(4 * (gi % 2), 4 * (gi % 2) + 4)) if gi < 2 else banks[gi - 2]
-        if gi >= 2:
-            m = len(groups[gi - 2])
-            bs = bs[m:] + bs[:m]
-        banks.append(bs)
-        pvbank += bs[:len(sl)]
-    free = {k: [] for k in range(8)}
-    tS, tSub, tE, tQ, tPV, tEv, tC, tCo, tK = {}, {}, {}, {}, {}, {}, {}, {}, {}
-
-    def cols(gi):
-        s = groups[gi]
-        return 128 * s[0], 128 * len(s)
-
-    def scores(gi):
-        o, n = cols(gi)
-        deps = [t_q if s == 0 else ("q%d" % rk[s], 16) for s in groups[gi]]
-        for b in range(4):
-            k = banks[gi][b]
-            tS[gi, b] = op("t", lambda e: e.matmul_mx(bank(k, n), T.kc[:, 128 * b:128 * b + 128], T.ks[:, 128 * b:128 * b + 128],
-                                                      T.qc[:, o:o + n], T.qs[:, o:o + n], True, True), deps + [t_k[b]] + free[k])
-
-    def first(gi):
-        o, n = cols(gi)
-        tC[gi] = op("s", lambda e: e.activation(T.s0[:, o:o + n], bank(banks[gi][0], n), AF.Copy), [tS[gi, 0]])
-
-    def shift(gi):
-        o, n = cols(gi)
-        nb = n // 32
-        h = {}
-        ps = [128 * x for x in groups[gi]]
-
-        def mx(p, c):
-            def f():
-                in0 = (T.s0 if c == 1 else T.mx)[:, p:p + 128]
-                k = 512 * banks[gi][c] + p - o
-                h[p] = op("v", lambda e: e.tensor_tensor((T.mb if c == 3 else T.mx)[:, p:p + 128], in0, T.ps[:, k:k + 128], mxm),
-                          [tC[gi] if c == 1 else h[p], tS[gi, c]])
-            return f
-
-        def tr(p):
-            def f():
-                h[p] = op("v", lambda e: e.transpose(T.mt[:, p:p + 128], T.mb[:, p:p + 128]), [h[p]])
-            return f
-
-        def sc(p):
-            def f():
-                h[p] = op("v", lambda e: e.tensor_tensor_scan(T.sc[:, p:p + 128], T.d0[:, 0:128], T.mt[:, p:p + 128], LOW, add, mxm), [h[p], t_d])
-            return f
-
-        def xh():
-            h["x"] = op("v", lambda e: e.tensor_tensor(T.xh[0:64, o // 32:o // 32 + nb], T.sc[0:64, o + 31:o + n:32], T.sc[64:128, o + 31:o + n:32], mxm),
-                        [h[p] for p in ps])
-
-        def vq(a):
-            def f():
-                h["z"] = op("v", lambda e: e.tensor_tensor(T.zz[32 * a:32 * a + 32, o:o + n:32], T.xh[0:32, o // 32:o // 32 + nb],
-                                                           T.xh[32:64, o // 32:o // 32 + nb], mxm), [h["x"], t_z])
-            return f
-
-        def fi(p):
-            def f():
-                h[p] = op("v", lambda e: e.tensor_tensor_scan(T.fi[:, p:p + 128], T.d0[:, 0:128], T.zz[:, p:p + 128], LOW, add, mxm), [h["z"]])
-            return f
-
-        def t2(p):
-            def f():
-                tC[gi, "b"] = op("v", lambda e: e.transpose(T.cb[:, p:p + 128], T.fi[:, p:p + 128]), [h[p]])
-            return f
-
-        def co(x):
-            def f():
-                for out in [T.co[:, 4 * rk[x]:4 * rk[x] + 4]] + ([T.cl[:, 4 * rank:4 * rank + 4]] if x == 0 else []):
-                    tCo[gi] = op("s", lambda e: e.activation(out, T.zz[:, 128 * x:128 * x + 128:32], AF.Copy, bias=SLACK, scale=A), [h["z"], t_c])
-            return f
-
-        return ([mx(p, c) for c in (1, 2, 3) for p in ps] + [tr(p) for p in ps] + [sc(p) for p in ps] + [xh],
-                [vq(a) for a in range(4)], [fi(p) for p in ps], [co(x) for x in groups[gi]], [t2(p) for p in ps])
-
-    pend = []
-
-    def subtract(gi, b):
-        o, n = cols(gi)
-        k = banks[gi][b]
-        y = 4 * o + b * n
-        tSub[gi, b] = op("v", lambda e: e.tensor_tensor(T.yy[:, y:y + n], bank(k, n), T.cb[:, o:o + n], sub), [tC[gi, "b"]])
-        free[k] = [tSub[gi, b]]
-
-    def relu(gi, b):
-        o, n = cols(gi)
-        y = 4 * o + b * n
-        t = None
-        if not VCLAMP[gi]:
-            t = op("s", lambda e: e.activation(T.rr[:, y:y + n], T.yy[:, y:y + n], AF.Relu, bias=20.0 - SLACK, scale=A), [tSub[gi, b]])
-        pend.append((gi, b, t))
-
-    def expo():
-        gi, b, t = pend.pop(0)
-        o, n = cols(gi)
-        y = 4 * o + b * n
-        out = T.pt[:, 4 * o + b:4 * o + 4 * n:4]
-        if t is None:
-            tE[gi] = op("s", lambda e: e.activation(out, T.yy[:, y:y + n], AF.Exp, bias=-SLACK, scale=A), [tSub[gi, b]])
-        else:
-            tE[gi] = op("s", lambda e: e.activation(out, T.rr[:, y:y + n], AF.Exp, bias=-20.0), [t])
-
+    t_v = []
+    tS, tCp, tM, tB, tE, tT, tP, tQ, tPV, tEv, tCo = {}, {}, {}, {}, {}, {}, {}, {}, {}, {}, {}
+    pvb = {s: (6 + s if s < 2 else s - 2) for s in range(NR)}
     nst = [0]
 
-    def store(out, in_, deps):
-        need("y", deps)
-        g.sync.dma_start(out, in_).then_inc(sem["st"], 16)
+    def load_v():
+        t_v.append(op("v", lambda e: e.quantize_mx(T.vc[:, 0:128], T.vs[:, 0:128], T.vin[:]), [("lv", 16)]))
+
+    def score(s):
+        deps = [t_q if s == 0 else ("q%d" % rk[s], 16)]
+        tS[s] = op("t", lambda e: e.matmul_mx(bank(s, 0, 512), T.qc[:, 128 * s:128 * s + 128], T.qs[:, 128 * s:128 * s + 128],
+                                              T.kc[:, 0:512], T.ks[:, 0:512], True, True), deps + t_k)
+
+    def half(s):
+        tCp[s] = op("s", lambda e: e.activation(T.s0[:, 256 * s:256 * s + 256], bank(s, 0, 256), AF.Copy), [tS[s]])
+
+    def maximum(s):
+        tM[s] = op("v", lambda e: e.tensor_tensor_scan(T.fm[:, 256 * s:256 * s + 256], T.s0[:, 256 * s:256 * s + 256], bank(s, 256, 512), LOW, mxm, mxm),
+                   [tCp[s], tS[s]])
+
+    def shift(s):
+        m = T.fm[:, 256 * s + 255:256 * s + 256]
+        tB[s] = op("s", lambda e: e.activation(T.nb[:, s:s + 1], m, AF.Copy, scale=-A), [tM[s]])
+        tCo[s] = op("s", lambda e: e.activation(T.cc[:, rk[s]:rk[s] + 1], m, AF.Copy, scale=A), [tM[s], t_c])
+        if s == 0:
+            tCo[s] = op("s", lambda e: e.activation(T.cl[:, 4 * rank:4 * rank + 1], m, AF.Copy, scale=A), [tM[s]])
+
+    def expo(s):
+        for b in range(4):
+            tE[s] = op("s", lambda e: e.activation(T.ee[:, 4 * s:4 * s + 4, 32 * b:32 * b + 32], T.ps[:, 512 * s + b:512 * s + 512:4], AF.Exp,
+                                                   bias=T.nb[:, s:s + 1], scale=A), [tB[s], tM[s]])
+
+    def turn(s):
+        c = 1024 * (s // 2)
+        for b in range(4):
+            tT[s] = op("v", lambda e: e.transpose(T.zz[:, c + 4 * (s % 2) + b:c + 1024:8], T.ee[:, 4 * s + b, :]), [tE[s]])
+
+    def moves(s):
+        need("y", [tT[s], tT[s + 1]])
+        for a in range(4):
+            g.sync.dma_start(T.yy[:, 512 * s + 256 * a:512 * s + 256 * a + 256], T.zz[32 * a:32 * a + 32, 512 * s:512 * s + 1024]).then_inc(sem["y%d" % s], 16)
+
+    def clamp(s):
+        c = 1024 * (s // 2)
+        for b in range(4):
+            tP[s] = op("v", lambda e: e.tensor_scalar(T.pt[:, 512 * s + b:512 * s + 512:4], T.yy[:, c + 4 * (s % 2) + b:c + 1024:8], FLOOR, None, mxm),
+                       [("y%d" % (s - s % 2), 64)])
+
+    def quant(s):
+        tQ[s] = op("v", lambda e: e.quantize_mx(T.pc[:, 128 * s:128 * s + 128], T.pp[:, 128 * s:128 * s + 128], T.pt[:, 512 * s:512 * s + 512]), [tP[s]])
+
+    def values(s):
+        tPV[s] = op("t", lambda e: e.matmul_mx(bank(pvb[s], 0, 256), T.pc[:, 128 * s:128 * s + 128], T.pp[:, 128 * s:128 * s + 128],
+                                               T.vc[:, 0:256], T.vs[:, 0:256], True, True), [tQ[s], t_v[0], t_V1] + ([tE[s - 2]] if s >= 2 else []))
+
+    def evac(s):
+        tEv[s] = op("s", lambda e: e.activation(T.sr[:, RW * s:RW * s + RN], bank(pvb[s], 0, RN), AF.Copy), [tPV[s]])
+
+    def store(out, in_, deps, q="y"):
+        need(q, deps)
+        (g.sync if q == "y" else g.scalar).dma_start(out, in_).then_inc(sem["st"], 16)
         nst[0] += 16
-
-    def quant(gi):
-        for s in groups[gi]:
-            tK[s] = tE[gi]
-            if VCLAMP[gi]:
-                tK[s] = op("v", lambda e: e.tensor_scalar(T.pt[:, 512 * s:512 * s + 512], T.pt[:, 512 * s:512 * s + 512], FLOOR, None, mxm), [tE[gi]])
-        for s in groups[gi]:
-            tQ[s] = op("v", lambda e: e.quantize_mx(T.pc[:, 128 * s:128 * s + 128], T.pp[:, 128 * s:128 * s + 128], T.pt[:, 512 * s:512 * s + 512]), [tK[s]])
-            store(T.p[rk[s]], T.pt[:, 512 * s:512 * s + 512], [tK[s]])
-
-    def values(gi):
-        for s in groups[gi]:
-            k = pvbank[s]
-            tPV[s] = op("t", lambda e: e.matmul_mx(bank(k, 256), T.pc[:, 128 * s:128 * s + 128], T.pp[:, 128 * s:128 * s + 128],
-                                                   T.vc[:, 0:256], T.vs[:, 0:256], True, True), [tQ[s], t_v, t_V1] + free[k])
-
-    def evac(gi):
-        for s in groups[gi]:
-            tEv[s] = op("s", lambda e: e.activation(T.sr[:, RW * s:RW * s + RN], bank(pvbank[s], RN), AF.Copy), [tPV[s]])
-            free[pvbank[s]] = [tEv[s]]
 
     def hk(b):
         h = relay[(core, b)]
         return h, [x for x in me if relay.get((core, x)) == h].index(b)
 
-    def send_c(gi):
-        need("g", [tCo[gi]])
+    def send_c(slots):
+        need("g", [tCo[s] for s in slots])
         trs, on = [], {}
-        for s in [s for s in groups[gi] if s]:
-            b, to, land, name = me[s], me[s], T.cl[:, 4 * rank:4 * rank + 4], "carr"
+        for s in slots:
+            b, to, land, name = me[s], me[s], T.cl[:, 4 * rank:4 * rank + 1], "carr"
             if (core, b) in relay:
                 to, k = hk(b)
-                land, name = T.hl[:, 4 * k:4 * k + 4], "hc%d" % k
+                land, name = T.hl[:, 4 * k:4 * k + 1], "hc%d" % k
             n, k = lane(to, 4)
             on[k] = on.get(k, -1) + 1
             trs.append(RemoteDMATransfer(dst_ids=[dest(topo, to)], dma_engine_mask=engines(topo.mask(core, to), n, k + on[k]), remote_sem=sem[name],
-                                         srcs=[T.co[:, 4 * rk[s]:4 * rk[s] + 4]], dsts=[land]))
+                                         srcs=[T.cc[:, rk[s]:rk[s] + 1]], dsts=[land]))
             sent[0] += n
         g.remote_dma_fused(trs, local_sem=sem["sent"])
 
-    def send_a(gi):
-        for s in [s for s in groups[gi] if s]:
-            b, src = me[s], T.sr[:, RW * s:RW * s + RN]
-            need("g", [tEv[s]])
-            if (core, b) in relay:
-                h, k = hk(b)
-                send(src, [(h, T.ha[:, RW * k:RW * k + RN])], "ha%d" % k, *lane(h, 8))
-            else:
-                send(src, [(b, T.ar[:, RW * rank:RW * rank + RN])], "a%d" % rank, *lane(b, 8))
+    def send_a(s):
+        b, src = me[s], T.sr[:, RW * s:RW * s + RN]
+        need("g", [tEv[s]])
+        if (core, b) in relay:
+            h, k = hk(b)
+            send(src, [(h, T.ha[:, RW * k:RW * k + RN])], "ha%d" % k, *lane(h, 8))
+        else:
+            send(src, [(b, T.ar[:, RW * rank:RW * rank + RN])], "a%d" % rank, *lane(b, 8))
 
-    scores(0)
-    first(0)
-    up, vq, fi, co, t2 = shift(0)
-    run(up[:-1])
-    t_v = op("v", lambda e: e.quantize_mx(T.vc[:, 0:128], T.vs[:, 0:128], T.vin[:]), [("lv", 16)])
-    run(up[-1:]), run(vq), run(fi), run(co), run(t2)
-    scores(1)
-    for gi in range(ng):
-        last = gi == ng - 1
-        if not last:
-            up, vq, fi, co, t2 = shift(gi + 1)
-        if gi and not last:
-            evac(gi - 1)
-            send_a(gi - 1)
-            scores(gi + 1)
-        for b in range(4):
-            subtract(gi, b), relu(gi, b)
-            if b:
-                expo()
-            if b == 0 and not last:
-                first(gi + 1)
-        expo()
-        if not last:
-            early = EARLY if gi == ng - 2 else len(up)
-            run(up[:early])
-            if gi == ng - 2:
-                quant(gi), values(gi), evac(gi), send_a(gi)
-            run(up[early:]), run(vq), run(co)
-            send_c(gi + 1)
-            run(fi)
-            if gi < ng - 2:
-                quant(gi), values(gi)
-            run(t2)
-    quant(ng - 1), values(ng - 1), evac(ng - 1), send_a(ng - 1)
+    steps = dict(S=score, h=half, m=maximum, b=shift, e=expo, t=turn, Y=moves, c=clamp, q=quant, x=values, v=evac, A=send_a)
+    for w in PLAN.split():
+        slots = [int(x) for x in w[1:]]
+        if w[0] == "V":
+            load_v()
+        elif w[0] == "C":
+            send_c(slots)
+        else:
+            for s in slots:
+                steps[w[0]](s)
 
-    t_ct = op("v", lambda e: e.transpose(T.ct[0:32, :], T.co[0:32, :]), [tCo[gi] for gi in range(ng)])
-    store(T.c[:], T.ct[0:24, :], [t_ct])
-
-    tw = []
+    t_ct = op("v", lambda e: e.transpose(T.ct[:], T.cc[:]), [tCo[s] for s in range(NR)])
     for b in range(4):
-        tw.append(op("v", lambda e: e.tensor_reduce(T.nm[32 * b:32 * b + 32, 0:1], T.cl[32 * b:32 * b + 32, b:24:4], AxisListType.X, mxm, negate=True),
-                     [("carr", 20), tCo[0]]))
-    tw = [op("s", lambda e: e.activation(T.wt[32 * b:32 * b + 32, 0:6], T.cl[32 * b:32 * b + 32, b:24:4], AF.Exp, bias=T.nm[32 * b:32 * b + 32, 0:1]),
-             [tw[b], t_w, ("carr", 20), tCo[0]]) for b in range(4)]
-    t_wo = op("v", lambda e: e.transpose(T.wo[:], T.wt[:]), tw)
+        store(T.c[:, 32 * b:32 * b + 32], T.ct[32 * b:32 * b + 6, :], [t_ct])
+
+    t_nm = op("v", lambda e: e.tensor_reduce(T.nm[:, 0:1], T.cl[:, 0:24:4], AxisListType.X, mxm, negate=True), [("carr", 20), tCo[0]])
+    t_wt = op("s", lambda e: e.activation(T.wt[:, 0:6], T.cl[:, 0:24:4], AF.Exp, bias=T.nm[:, 0:1]), [t_nm, t_w, ("carr", 20)])
+    t_wo = op("v", lambda e: e.transpose(T.wo[:], T.wt[:]), [t_wt])
     for b in range(4):
         store(T.w[:, 32 * b:32 * b + 32], T.wo[32 * b:32 * b + 6, :], [t_wo])
+    for s in range(NR):
+        store(T.p[rk[s]], T.pt[:, 512 * s:512 * s + 512], [tP[s]])
 
     def when(j):
-        return group_of[order[j].index(core)] + 1.5 * ((j, core) in relay), j
+        return DONE[order[j].index(core)] + HOP * ((j, core) in relay), j
 
     acc = None
     for k, j in enumerate([core] + sorted([j for j in cores if j != core], key=when)):
         r = T.rank_of(j)
-        src = T.sr[:, 0:RN] if k == 0 else T.ar[:, RW * r:RW * r + RN]
-        out = T.ac[:, 0:RN] if k == 0 else T.uu[:, RW * r:RW * r + RN]
-        t = op("s", lambda e: e.activation(out, src, AF.Copy, scale=T.wt[:, r:r + 1]), tw + ([tEv[0]] if k == 0 else [("a%d" % r, 8)]))
-        acc = t if k == 0 else op("v", lambda e: e.tensor_tensor(T.ac[:, 0:RN], T.ac[:, 0:RN], T.uu[:, RW * r:RW * r + RN], add), [acc, t])
-    t_rc = op("v", lambda e: e.reciprocal(T.rc[:, 0:1], T.ac[:, 128:129]), [acc])
-    t_on = op("v", lambda e: e.tensor_scalar(T.on[:], T.ac[:, 0:128], T.rc[:, 0:1], None, mul), [t_rc])
+        w, o = T.wt[:, r:r + 1], RW * r
+        here = [t_wt] + ([tEv[0]] if k == 0 else [("a%d" % r, 8)])
+        if k < NR - 1:
+            src = T.sr[:, 0:RN] if k == 0 else T.ar[:, o:o + RN]
+            out = T.ac[:, 0:RN] if k == 0 else T.uu[:, o:o + RN]
+            t = op("s", lambda e: e.activation(out, src, AF.Copy, scale=w), here)
+            acc = t if k == 0 else op("v", lambda e: e.tensor_tensor(T.ac[:, 0:RN], T.ac[:, 0:RN], T.uu[:, o:o + RN], add), [acc, t])
+        else:
+            t = op("v", lambda e: e.tensor_scalar(T.rc[:, 1:2], T.ar[:, o + 128:o + 129], w, T.ac[:, 128:129], mul, add), here + [acc])
+            t_rc = op("v", lambda e: e.reciprocal(T.rc[:, 0:1], T.rc[:, 1:2]), [t])
+            tu = [op("s", lambda e: e.activation(T.uu[:, o + h:o + h + 64], T.ar[:, o + h:o + h + 64], AF.Copy, scale=w), here) for h in (0, 64)]
+            ta = [op("v", lambda e: e.tensor_tensor(T.ac[:, h:h + 64], T.ac[:, h:h + 64], T.uu[:, o + h:o + h + 64], add), [acc, tu[h // 64]]) for h in (0, 64)]
+            ton = [op("v", lambda e: e.tensor_scalar(T.on[:, h:h + 64], T.ac[:, h:h + 64], T.rc[:, 0:1], None, mul), [t_rc, ta[h // 64]]) for h in (0, 64)]
     for b in range(4):
         for a in range(4):
-            t = op("v", lambda e: e.transpose(T.ot[32 * b:32 * b + 32, 32 * a:32 * a + 32], T.on[32 * a:32 * a + 32, 32 * b:32 * b + 32]), [t_on])
-        store(T.o[32 * b:32 * b + 32, :], T.ot[32 * b:32 * b + 32, :], [t])
+            t = op("v", lambda e: e.transpose(T.ot[32 * b:32 * b + 32, 32 * a:32 * a + 32], T.on[32 * a:32 * a + 32, 32 * b:32 * b + 32]), [ton[b // 2]])
+        store(T.o[32 * b:32 * b + 32, :], T.ot[32 * b:32 * b + 32, :], [t], "ys"[b % 2])
 
     g.sync.wait_ge(sem["st"], nst[0])
+    for s in (0, 2, 4):
+        need("g", [("y%d" % s, 64)])
     need("g", [(q, count[q]) for q in count])
     g.wait_ge(sem["sent"], sent[0])

@@ -18,25 +18,25 @@ SCRATCH = {
     "vc": ("sbuf", [128, 256], "float8_e4m3fn_x4"), "vs": ("sbuf", [128, 256], "uint8"),
     "pc": ("sbuf", [128, 768], "float8_e4m3fn_x4"), "pp": ("sbuf", [128, 768], "uint8"),
     "pt": ("sbuf", [128, 3072], "bfloat16"),
-    "s0": ("sbuf", [128, 1536], "float32"), "fm": ("sbuf", [128, 1536], "float32"), "nb": ("sbuf", [128, 8], "float32"),
-    "ee": ("sbuf", [128, 24, 128], "bfloat16"), "zz": ("sbuf", [128, 3072], "bfloat16"), "yy": ("sbuf", [128, 3072], "bfloat16"),
+    "s0": ("sbuf", [128, 1536], "float32"), "fm": ("sbuf", [128, 1536], "float32"), "nb": ("sbuf", [128, 32], "float32"),
+    "ee": ("sbuf", [128, 24, 128], "bfloat16"), "zz": ("sbuf", [128, 3072], "bfloat16"), "yy": ("sbuf", [128, 384, 8], "bfloat16"),
     "cc": ("sbuf", [128, 32], "float32"), "ct": ("sbuf", [128, 32], "float32"), "cl": ("sbuf", [128, 24], "float32"),
     "nm": ("sbuf", [128, 4], "float32"), "wt": ("sbuf", [128, 32], "float32"), "wo": ("sbuf", [128, 32], "float32"),
     "sr": ("sbuf", [128, NR * RW], "float32"), "ar": ("sbuf", [128, NR * RW], "float32"), "uu": ("sbuf", [128, NR * RW], "float32"),
-    "ac": ("sbuf", [128, RW], "float32"), "rc": ("sbuf", [128, 4], "float32"), "on": ("sbuf", [128, 128], "float32"),
-    "ot": ("sbuf", [128, 128], "float32"),
+    "ac": ("sbuf", [128, RW], "float32"), "ap": ("sbuf", [128, 128], "float32"), "rc": ("sbuf", [128, 4], "float32"),
+    "on": ("sbuf", [128, 128], "float32"), "ot": ("sbuf", [128, 128], "float32"),
     "hc": ("sbuf", [128, 128], "float8_e4m3fn_x4"), "hs": ("sbuf", [128, 128], "uint8"),
     "hl": ("sbuf", [128, 8], "float32"), "ha": ("sbuf", [128, 2 * RW], "float32"),
     "ps": ("psum", [128, 4096], "float32"),
 }
-SEMAPHORES = (["v", "s", "t", "lq", "lv", "st", "sent", "carr", "hqc", "hqs", "hc0", "hc1", "ha0", "ha1", "y0", "y2", "y4"]
-              + ["lk%d" % b for b in range(4)] + ["q%d" % i for i in range(NR)] + ["a%d" % i for i in range(NR)])
+SEMAPHORES = (["v", "s", "t", "lq", "lv", "st", "sent", "carr", "hqc", "hqs", "hc0", "hc1", "ha0", "ha1", "y0", "y2", "y4", "lk0", "lk1"]
+              + ["q%d" % i for i in range(NR)] + ["a%d" % i for i in range(NR)])
 
 GROUP = (0, 1, 2, 2, 3, 3)
-DONE = (0, 1.6, 0, 0.7, 2.5, 3.1)
-HOP = 2.0
-PLAN = """S0 h0 m0 V b0 e0 S1 h1 t0 m1 b1 e1 S2 S3 C1 t1 Y0 h2 h3 m2 m3 b2 e2 b3 C23 e3 t2 t3 Y2 S4 S5 h4 h5 m4 m5 b4 e4 b5 C45 e5 t4 t5 Y4
-c2 q2 x2 c3 q3 x3 v23 A23 c10 q10 x10 v10 A1 c4 q4 x4 c5 q5 x5 v45 A45"""
+DONE = (0, 0.4, 0.2, 0.7, 2.5, 3.1)
+HOP = 0.5
+PLAN = """S0 h0 m0 V b0 o0 S1 S2 S3 e0 M1 t0 b1 C1 e1 M2 t1 Y0 M3 b2 e2 b3 C23 e3 t2 t3 Y2 S4 S5 h4 m4 M5 c1 q1 b4 e4 b5 C45 e5 x1
+t4 t5 Y4 c2 q2 x2 v2 A2 v1 A1 c3 q3 x3 v3 A3 c4 q4 x4 v4 A4 c5 q5 x5 v5 A5 c0 q0 x0 v0"""
 
 
 def engines(mask, n, k=0):
@@ -95,7 +95,7 @@ def make_plan(T, topo):
         mate = [i for i in cores if i != j and topo.chip(i) == topo.chip(j)]
         rest = [i for i in cores if i != j and i not in mate]
         rest.sort(key=lambda i: ((i, j) in relay, (j, i) not in relay, i))
-        late = sorted(rest[2:], key=lambda i: ((i, j) in relay and first[(i, relay[(i, j)])] != j, i))
+        late = sorted(rest[2:], key=lambda i: ((i, j) in relay and first[(i, relay[(i, j)])] != j, (j, i) not in relay, i))
         order[j] = [j] + mate + rest[:2] + late
     return relay, order, first
 
@@ -119,6 +119,9 @@ def rank_program(g, core, T, topo):
         g.remote_dma_fused([RemoteDMATransfer(dst_ids=[dest(topo, c) for c, _ in pieces], dma_engine_mask=m, remote_sem=sem[rsem],
                                               srcs=[src], dsts=[p for _, p in pieces])], local_sem=sem["sent"])
         sent[0] += n
+
+    def width(a, b):
+        return bin(topo.mask(a, b)).count("1")
 
     def codes(buf, a, b):
         return buf[:, a:b].bitcast(dt.uint8)
@@ -152,8 +155,8 @@ def rank_program(g, core, T, topo):
             g.wait_ge(sem["hc%d" % k], 4)
             send(T.hl[:, 4 * k:4 * k + 1], [(b, T.cl[:, 4 * sr:4 * sr + 1])], "carr", 4)
         for k, b in enumerate(dsts):
-            g.wait_ge(sem["ha%d" % k], 8)
-            send(T.ha[:, RW * k:RW * k + RN], [(b, T.ar[:, RW * sr:RW * sr + RN])], "a%d" % sr, 8)
+            g.wait_ge(sem["ha%d" % k], width(src, core))
+            send(T.ha[:, RW * k:RW * k + RN], [(b, T.ar[:, RW * sr:RW * sr + RN])], "a%d" % sr, width(core, b))
         g.wait_ge(sem["sent"], sent[0])
         return
 
@@ -185,14 +188,14 @@ def rank_program(g, core, T, topo):
 
     g.sync.dma_start(T.qin[:, 0:256], T.q[:, 0:256]).then_inc(sem["lq"], 16)
     g.scalar.dma_start(T.qin[:, 256:512], T.q[:, 256:512]).then_inc(sem["lq"], 16)
-    for b in range(4):
-        (g.scalar if b % 2 == 0 else g.sync).dma_start(T.kin[:, 512 * b:512 * b + 512], T.k[:, 512 * b:512 * b + 512]).then_inc(sem["lk%d" % b], 16)
-    g.scalar.dma_start(T.vin[:], T.v[:]).then_inc(sem["lv"], 16)
+    for b in range(2):
+        (g.sync if b else g.scalar).dma_start(T.kin[:, 1024 * b:1024 * b + 1024], T.k[:, 1024 * b:1024 * b + 1024]).then_inc(sem["lk%d" % b], 16)
+    g.sync.dma_start(T.vin[:], T.v[:]).then_inc(sem["lv"], 16)
 
     t_zer = op("v", lambda e: e.memset(T.zer[:], 0.0), [])
     t_one = op("s", lambda e: e.activation(T.one[:], T.zer[:], AF.Exp), [t_zer])
     t_w = op("v", lambda e: e.memset(T.wt[:], 0.0), [])
-    t_c = op("v", lambda e: e.memset(T.cc[:], 0.0), [])
+    t_c = op("v", lambda e: e.memset(T.nb[:], 0.0), [])
 
     t_q = op("v", lambda e: e.quantize_mx(T.qc[:, 0:128], T.qs[:, 0:128], T.qin[:]), [("lq", 32)])
     need("g", [t_q])
@@ -210,8 +213,8 @@ def rank_program(g, core, T, topo):
         for _ in put_q(core, [b], T.qc, T.qs, "q%d" % rank, *lane(b, 8)):
             pass
     t_V1 = op("v", lambda e: e.quantize_mx(T.vc[:, 128:256], T.vs[:, 128:256], T.one[:]), [t_one])
-    t_k = [op("v", lambda e: e.quantize_mx(T.kc[:, 128 * b:128 * b + 128], T.ks[:, 128 * b:128 * b + 128], T.kin[:, 512 * b:512 * b + 512]),
-              [("lk%d" % b, 16)]) for b in range(4)]
+    t_k = [op("v", lambda e: e.quantize_mx(T.kc[:, 256 * b:256 * b + 256], T.ks[:, 256 * b:256 * b + 256], T.kin[:, 1024 * b:1024 * b + 1024]),
+              [("lk%d" % b, 16)]) for b in range(2)]
     t_v = []
     tS, tCp, tM, tB, tE, tT, tP, tQ, tPV, tEv, tCo = {}, {}, {}, {}, {}, {}, {}, {}, {}, {}, {}
     pvb = {s: (6 + s if s < 2 else s - 2) for s in range(NR)}
@@ -232,17 +235,20 @@ def rank_program(g, core, T, topo):
         tM[s] = op("v", lambda e: e.tensor_tensor_scan(T.fm[:, 256 * s:256 * s + 256], T.s0[:, 256 * s:256 * s + 256], bank(s, 256, 512), LOW, mxm, mxm),
                    [tCp[s], tS[s]])
 
+    def maximum_alone(s):
+        tM[s] = op("v", lambda e: e.tensor_reduce(T.fm[:, 256 * s + 255:256 * s + 256], bank(s, 0, 512), AxisListType.X, mxm), [tS[s]])
+
     def shift(s):
         m = T.fm[:, 256 * s + 255:256 * s + 256]
-        tB[s] = op("s", lambda e: e.activation(T.nb[:, s:s + 1], m, AF.Copy, scale=-A), [tM[s]])
-        tCo[s] = op("s", lambda e: e.activation(T.cc[:, rk[s]:rk[s] + 1], m, AF.Copy, scale=A), [tM[s], t_c])
-        if s == 0:
-            tCo[s] = op("s", lambda e: e.activation(T.cl[:, 4 * rank:4 * rank + 1], m, AF.Copy, scale=A), [tM[s]])
+        tB[s] = op("s", lambda e: e.activation(T.nb[:, rk[s]:rk[s] + 1], m, AF.Copy, scale=-A), [tM[s], t_c])
+
+    def own(s):
+        tCo[s] = op("s", lambda e: e.activation(T.cl[:, 4 * rank:4 * rank + 1], T.nb[:, rank:rank + 1], AF.Copy), [tB[s]])
 
     def expo(s):
         for b in range(4):
             tE[s] = op("s", lambda e: e.activation(T.ee[:, 4 * s:4 * s + 4, 32 * b:32 * b + 32], T.ps[:, 512 * s + b:512 * s + 512:4], AF.Exp,
-                                                   bias=T.nb[:, s:s + 1], scale=A), [tB[s], tM[s]])
+                                                   bias=T.nb[:, rk[s]:rk[s] + 1], scale=A), [tB[s], tM[s]])
 
     def turn(s):
         c = 1024 * (s // 2)
@@ -250,15 +256,16 @@ def rank_program(g, core, T, topo):
             tT[s] = op("v", lambda e: e.transpose(T.zz[:, c + 4 * (s % 2) + b:c + 1024:8], T.ee[:, 4 * s + b, :]), [tE[s]])
 
     def moves(s):
-        need("y", [tT[s], tT[s + 1]])
+        for q in "ys" if s == 4 else "y":
+            need(q, [tT[s], tT[s + 1]])
         for a in range(4):
-            g.sync.dma_start(T.yy[:, 512 * s + 256 * a:512 * s + 256 * a + 256], T.zz[32 * a:32 * a + 32, 512 * s:512 * s + 1024]).then_inc(sem["y%d" % s], 16)
+            (g.scalar if s == 4 and a % 2 else g.sync).dma_start(T.yy[:, 64 * s + 32 * a:64 * s + 32 * a + 32, :],
+                                                                 T.zz[32 * a:32 * a + 32, 512 * s:512 * s + 1024]).then_inc(sem["y%d" % s], 16)
 
     def clamp(s):
-        c = 1024 * (s // 2)
-        for b in range(4):
-            tP[s] = op("v", lambda e: e.tensor_scalar(T.pt[:, 512 * s + b:512 * s + 512:4], T.yy[:, c + 4 * (s % 2) + b:c + 1024:8], FLOOR, None, mxm),
-                       [("y%d" % (s - s % 2), 64)])
+        c, h = 128 * (s // 2), 4 * (s % 2)
+        tP[s] = op("v", lambda e: e.tensor_scalar(T.pt[:, 512 * s:512 * s + 512], T.yy[:, c:c + 128, h:h + 4], FLOOR, None, mxm),
+                   [("y%d" % (s - s % 2), 64)])
 
     def quant(s):
         tQ[s] = op("v", lambda e: e.quantize_mx(T.pc[:, 128 * s:128 * s + 128], T.pp[:, 128 * s:128 * s + 128], T.pt[:, 512 * s:512 * s + 512]), [tP[s]])
@@ -280,7 +287,7 @@ def rank_program(g, core, T, topo):
         return h, [x for x in me if relay.get((core, x)) == h].index(b)
 
     def send_c(slots):
-        need("g", [tCo[s] for s in slots])
+        need("g", [tB[s] for s in slots])
         trs, on = [], {}
         for s in slots:
             b, to, land, name = me[s], me[s], T.cl[:, 4 * rank:4 * rank + 1], "carr"
@@ -290,7 +297,7 @@ def rank_program(g, core, T, topo):
             n, k = lane(to, 4)
             on[k] = on.get(k, -1) + 1
             trs.append(RemoteDMATransfer(dst_ids=[dest(topo, to)], dma_engine_mask=engines(topo.mask(core, to), n, k + on[k]), remote_sem=sem[name],
-                                         srcs=[T.cc[:, rk[s]:rk[s] + 1]], dsts=[land]))
+                                         srcs=[T.nb[:, rk[s]:rk[s] + 1]], dsts=[land]))
             sent[0] += n
         g.remote_dma_fused(trs, local_sem=sem["sent"])
 
@@ -299,11 +306,12 @@ def rank_program(g, core, T, topo):
         need("g", [tEv[s]])
         if (core, b) in relay:
             h, k = hk(b)
-            send(src, [(h, T.ha[:, RW * k:RW * k + RN])], "ha%d" % k, *lane(h, 8))
+            send(src, [(h, T.ha[:, RW * k:RW * k + RN])], "ha%d" % k, width(core, h))
         else:
-            send(src, [(b, T.ar[:, RW * rank:RW * rank + RN])], "a%d" % rank, *lane(b, 8))
+            send(src, [(b, T.ar[:, RW * rank:RW * rank + RN])], "a%d" % rank, width(core, b))
 
-    steps = dict(S=score, h=half, m=maximum, b=shift, e=expo, t=turn, Y=moves, c=clamp, q=quant, x=values, v=evac, A=send_a)
+    steps = dict(S=score, h=half, m=maximum, M=maximum_alone, b=shift, o=own, e=expo, t=turn, Y=moves, c=clamp, q=quant, x=values,
+                 v=evac, A=send_a)
     for w in PLAN.split():
         slots = [int(x) for x in w[1:]]
         if w[0] == "V":
@@ -314,12 +322,13 @@ def rank_program(g, core, T, topo):
             for s in slots:
                 steps[w[0]](s)
 
-    t_ct = op("v", lambda e: e.transpose(T.ct[:], T.cc[:]), [tCo[s] for s in range(NR)])
+    t_cc = op("s", lambda e: e.activation(T.cc[:], T.nb[:], AF.Copy, scale=-1.0), [tB[s] for s in range(NR)])
+    t_ct = op("v", lambda e: e.transpose(T.ct[:], T.cc[:]), [t_cc])
     for b in range(4):
         store(T.c[:, 32 * b:32 * b + 32], T.ct[32 * b:32 * b + 6, :], [t_ct])
 
-    t_nm = op("v", lambda e: e.tensor_reduce(T.nm[:, 0:1], T.cl[:, 0:24:4], AxisListType.X, mxm, negate=True), [("carr", 20), tCo[0]])
-    t_wt = op("s", lambda e: e.activation(T.wt[:, 0:6], T.cl[:, 0:24:4], AF.Exp, bias=T.nm[:, 0:1]), [t_nm, t_w, ("carr", 20)])
+    t_nm = op("v", lambda e: e.tensor_reduce(T.nm[:, 0:1], T.cl[:, 0:24:4], AxisListType.X, AluOpType.min), [("carr", 20), tCo[0]])
+    t_wt = op("s", lambda e: e.activation(T.wt[:, 0:6], T.cl[:, 0:24:4], AF.Exp, bias=T.nm[:, 0:1], scale=-1.0), [t_nm, t_w, ("carr", 20)])
     t_wo = op("v", lambda e: e.transpose(T.wo[:], T.wt[:]), [t_wt])
     for b in range(4):
         store(T.w[:, 32 * b:32 * b + 32], T.wo[32 * b:32 * b + 6, :], [t_wo])
@@ -333,22 +342,21 @@ def rank_program(g, core, T, topo):
     for k, j in enumerate([core] + sorted([j for j in cores if j != core], key=when)):
         r = T.rank_of(j)
         w, o = T.wt[:, r:r + 1], RW * r
-        here = [t_wt] + ([tEv[0]] if k == 0 else [("a%d" % r, 8)])
+        here = [t_wt] + ([tEv[0]] if k == 0 else [("a%d" % r, width(relay.get((j, core), j), core))])
         if k < NR - 1:
             src = T.sr[:, 0:RN] if k == 0 else T.ar[:, o:o + RN]
             out = T.ac[:, 0:RN] if k == 0 else T.uu[:, o:o + RN]
             t = op("s", lambda e: e.activation(out, src, AF.Copy, scale=w), here)
             acc = t if k == 0 else op("v", lambda e: e.tensor_tensor(T.ac[:, 0:RN], T.ac[:, 0:RN], T.uu[:, o:o + RN], add), [acc, t])
         else:
-            t = op("v", lambda e: e.tensor_scalar(T.rc[:, 1:2], T.ar[:, o + 128:o + 129], w, T.ac[:, 128:129], mul, add), here + [acc])
+            t = op("s", lambda e: e.activation(T.rc[:, 1:2], T.ar[:, o + 128:o + 129], AF.Identity, bias=T.ac[:, 128:129], scale=w), here + [acc])
             t_rc = op("v", lambda e: e.reciprocal(T.rc[:, 0:1], T.rc[:, 1:2]), [t])
-            tu = [op("s", lambda e: e.activation(T.uu[:, o + h:o + h + 64], T.ar[:, o + h:o + h + 64], AF.Copy, scale=w), here) for h in (0, 64)]
-            ta = [op("v", lambda e: e.tensor_tensor(T.ac[:, h:h + 64], T.ac[:, h:h + 64], T.uu[:, o + h:o + h + 64], add), [acc, tu[h // 64]]) for h in (0, 64)]
-            ton = [op("v", lambda e: e.tensor_scalar(T.on[:, h:h + 64], T.ac[:, h:h + 64], T.rc[:, 0:1], None, mul), [t_rc, ta[h // 64]]) for h in (0, 64)]
-    for b in range(4):
-        for a in range(4):
-            t = op("v", lambda e: e.transpose(T.ot[32 * b:32 * b + 32, 32 * a:32 * a + 32], T.on[32 * a:32 * a + 32, 32 * b:32 * b + 32]), [ton[b // 2]])
-        store(T.o[32 * b:32 * b + 32, :], T.ot[32 * b:32 * b + 32, :], [t], "ys"[b % 2])
+            tu = op("s", lambda e: e.activation(T.uu[:, o:o + 128], T.ar[:, o:o + 128], AF.Copy, scale=w), here)
+            ta = [op("v", lambda e: e.tensor_tensor(T.ap[:, 32 * b:32 * b + 32], T.ac[:, b:128:4], T.uu[:, o + b:o + 128:4], add), [acc, tu]) for b in range(4)]
+            ton = [op("v", lambda e: e.tensor_scalar(T.on[:, h:h + 64], T.ap[:, h:h + 64], T.rc[:, 0:1], None, mul), [t_rc, ta[h // 32 + 1]]) for h in (0, 64)]
+    tot = [op("v", lambda e: e.transpose(T.ot[:, h:h + 64], T.on[:, h:h + 64]), [ton[h // 64]]) for h in (0, 64)]
+    for a in range(4):
+        store(T.o[:, 32 * a:32 * a + 32], T.ot[32 * a:32 * a + 32, :], tot, "ys"[a % 2])
 
     g.sync.wait_ge(sem["st"], nst[0])
     for s in (0, 2, 4):

@@ -19,7 +19,8 @@ SCRATCH = {
     "pc": ("sbuf", [128, 768], "float8_e4m3fn_x4"), "pp": ("sbuf", [128, 768], "uint8"),
     "pt": ("sbuf", [128, 3072], "bfloat16"),
     "s0": ("sbuf", [128, 1536], "float32"), "fm": ("sbuf", [128, 1536], "float32"), "nb": ("sbuf", [128, 32], "float32"),
-    "ee": ("sbuf", [128, 24, 128], "bfloat16"), "zz": ("sbuf", [128, 3072], "bfloat16"), "yy": ("sbuf", [128, 384, 8], "bfloat16"),
+    "ee": ("sbuf", [128, 24, 128], "bfloat16"), "zz": ("sbuf", [128, 3072], "bfloat16"),
+    "yy": ("sbuf", [128, 256, 8], "bfloat16"), "y1": ("sbuf", [128, 1024], "bfloat16"),
     "cc": ("sbuf", [128, 32], "float32"), "ct": ("sbuf", [128, 32], "float32"), "cl": ("sbuf", [128, 24], "float32"),
     "nm": ("sbuf", [128, 4], "float32"), "wt": ("sbuf", [128, 32], "float32"), "wo": ("sbuf", [128, 32], "float32"),
     "sr": ("sbuf", [128, NR * RW], "float32"), "ar": ("sbuf", [128, NR * RW], "float32"), "uu": ("sbuf", [128, NR * RW], "float32"),
@@ -29,14 +30,15 @@ SCRATCH = {
     "hl": ("sbuf", [128, 8], "float32"), "ha": ("sbuf", [128, 2 * RW], "float32"),
     "ps": ("psum", [128, 4096], "float32"),
 }
-SEMAPHORES = (["v", "s", "t", "lq", "lv", "st", "sent", "carr", "hqc", "hqs", "hc0", "hc1", "ha0", "ha1", "y0", "y2", "y4", "lk0", "lk1"]
+SEMAPHORES = (["v", "s", "t", "lq", "lv", "st", "sent", "carr", "hqc", "hqs", "hc0", "hc1", "ha0", "ha1", "y0", "y2", "y4", "y5", "lk0", "lk1"]
               + ["q%d" % i for i in range(NR)] + ["a%d" % i for i in range(NR)])
 
-GROUP = (0, 1, 2, 2, 3, 3)
+PAIRED = 4
 DONE = (0, 0.4, 0.2, 0.7, 2.5, 3.1)
 HOP = 0.5
-PLAN = """S0 h0 m0 V b0 o0 S1 S2 S3 e0 M1 t0 b1 C1 e1 M2 t1 Y0 M3 b2 e2 b3 C23 e3 t2 t3 Y2 S4 S5 h4 m4 M5 c1 q1 b4 e4 b5 C45 e5 x1
-t4 t5 Y4 c2 q2 x2 v2 A2 v1 A1 c3 q3 x3 v3 A3 c4 q4 x4 v4 A4 c5 q5 x5 v5 A5 c0 q0 x0 v0"""
+PLAN = """k0 k1 S0 S1 h0 m0 I M1 b0 e0 S2 t0 b1 e1 S3 t1 h2 m2 M3 V o0 b2 e2 Y0 t2 b3 e3 t3 S4 h4 S5 m4 M5 c1 Y2 b4 e4 b5 e5 t4 q1 z4 t5 C1
+c2 C23 q2 x1 z5 x2 v1 C45 A1 c3 q3 v2 P3 c4 x3 q4 x4 v3 A2 A3 v4 c5 q5 x5 A4 v5 c0 q0 J A5 x0 N W j P2 O i P5 u0 u1 u2 +1 u3 +2 u4 +3 r4
+P0 P4 P1 +4 F"""
 
 
 def engines(mask, n, k=0):
@@ -84,20 +86,28 @@ def make_plan(T, topo):
                 load[l] = load.get(l, 0) + n
             for b in dsts:
                 relay[(a, b)] = best[1]
-    first, turns = {}, {}
+    first = {}
     for (a, b), h in sorted(relay.items()):
-        both = sorted(y for (x, y), z in relay.items() if (x, z) == (a, h))
-        if (a, h) not in first:
-            first[(a, h)] = min(both, key=lambda y: (turns.get(y, 0), y))
-            turns[first[(a, h)]] = turns.get(first[(a, h)], 0) + 1
-    order = {}
+        first[(a, h)] = min([y for (x, y), z in relay.items() if (x, z) == (a, h)], key=lambda y: ((y, a) not in relay, y))
+    mate, early, late, sends, order = {}, {}, {}, {}, {}
     for j in cores:
-        mate = [i for i in cores if i != j and topo.chip(i) == topo.chip(j)]
-        rest = [i for i in cores if i != j and i not in mate]
+        mate[j] = [i for i in cores if i != j and topo.chip(i) == topo.chip(j)]
+        rest = [i for i in cores if i != j and i not in mate[j]]
         rest.sort(key=lambda i: ((i, j) in relay, (j, i) not in relay, i))
-        late = sorted(rest[2:], key=lambda i: ((i, j) in relay and first[(i, relay[(i, j)])] != j, (j, i) not in relay, i))
-        order[j] = [j] + mate + rest[:2] + late
-    return relay, order, first
+        early[j], late[j] = rest[:2], rest[2:]
+    for j in cores:
+        far = [b for b in cores if b != j and b not in mate[j]]
+        rel = []
+        for b in far:
+            if (j, b) in relay and relay[(j, b)] not in rel:
+                rel.append(relay[(j, b)])
+        far = sorted([b for b in far if (j, b) not in relay], key=lambda b: (j not in early[b], (b, j) not in relay, b))
+        sends[j] = mate[j] + rel[::-1] + far
+    for j in cores:
+        early[j].sort(key=lambda i: ((j, i) not in relay, [b for b in sends[i] if b in cores].index(j), i))
+        late[j].sort(key=lambda i: ((i, j) not in relay, (i, j) in relay and first[(i, relay[(i, j)])] != j, -i))
+        order[j] = [j] + mate[j] + early[j] + late[j]
+    return relay, order, first, sends
 
 
 def dest(topo, c):
@@ -106,7 +116,7 @@ def dest(topo, c):
 
 
 def rank_program(g, core, T, topo):
-    relay, order, first = make_plan(T, topo)
+    relay, order, first, sends = make_plan(T, topo)
     cores = list(T.cores)
     sem = T.sem
     sent = [0]
@@ -186,10 +196,10 @@ def rank_program(g, core, T, topo):
 
     add, mul, mxm = AluOpType.add, AluOpType.mult, AluOpType.max
 
-    g.sync.dma_start(T.qin[:, 0:256], T.q[:, 0:256]).then_inc(sem["lq"], 16)
-    g.scalar.dma_start(T.qin[:, 256:512], T.q[:, 256:512]).then_inc(sem["lq"], 16)
+    g.sync.dma_start(T.qin[:], T.q[:]).then_inc(sem["lq"], 16)
     for b in range(2):
-        (g.sync if b else g.scalar).dma_start(T.kin[:, 1024 * b:1024 * b + 1024], T.k[:, 1024 * b:1024 * b + 1024]).then_inc(sem["lk%d" % b], 16)
+        g.sync.dma_start(T.kin[:, 1024 * b:1024 * b + 1024], T.k[:, 1024 * b:1024 * b + 1024]).then_inc(sem["lk%d" % b], 16)
+    need("y", [("lk1", 16)])
     g.sync.dma_start(T.vin[:], T.v[:]).then_inc(sem["lv"], 16)
 
     t_zer = op("v", lambda e: e.memset(T.zer[:], 0.0), [])
@@ -197,82 +207,89 @@ def rank_program(g, core, T, topo):
     t_w = op("v", lambda e: e.memset(T.wt[:], 0.0), [])
     t_c = op("v", lambda e: e.memset(T.nb[:], 0.0), [])
 
-    t_q = op("v", lambda e: e.quantize_mx(T.qc[:, 0:128], T.qs[:, 0:128], T.qin[:]), [("lq", 32)])
+    t_q = op("v", lambda e: e.quantize_mx(T.qc[:, 0:128], T.qs[:, 0:128], T.qin[:]), [("lq", 16)])
     need("g", [t_q])
-    mate = [b for b in cores if b != core and topo.chip(b) == topo.chip(core)]
-    far = [b for b in cores if b != core and b not in mate]
-    rel = []
-    for b in far:
-        if (core, b) in relay and relay[(core, b)] not in rel:
-            rel.append(relay[(core, b)])
-    far = sorted([b for b in far if (core, b) not in relay], key=lambda b: (GROUP[qslot(core, b)], (b, core) not in relay, b))
-    for h in reversed(rel):
-        send(codes(T.qc, 0, 128), [(h, codes(T.hc, 0, 128))], "hqc", *lane(h, 8))
-        send(T.qs[:, 0:128], [(h, T.hs[:, 0:128])], "hqs", *lane(h, 8))
-    for b in mate + far:
-        for _ in put_q(core, [b], T.qc, T.qs, "q%d" % rank, *lane(b, 8)):
-            pass
-    t_V1 = op("v", lambda e: e.quantize_mx(T.vc[:, 128:256], T.vs[:, 128:256], T.one[:]), [t_one])
-    t_k = [op("v", lambda e: e.quantize_mx(T.kc[:, 256 * b:256 * b + 256], T.ks[:, 256 * b:256 * b + 256], T.kin[:, 1024 * b:1024 * b + 1024]),
-              [("lk%d" % b, 16)]) for b in range(2)]
-    t_v = []
-    tS, tCp, tM, tB, tE, tT, tP, tQ, tPV, tEv, tCo = {}, {}, {}, {}, {}, {}, {}, {}, {}, {}, {}
+    for b in sends[core]:
+        if b in cores:
+            for _ in put_q(core, [b], T.qc, T.qs, "q%d" % rank, *lane(b, 8)):
+                pass
+        else:
+            send(codes(T.qc, 0, 128), [(b, codes(T.hc, 0, 128))], "hqc", *lane(b, 8))
+            send(T.qs[:, 0:128], [(b, T.hs[:, 0:128])], "hqs", *lane(b, 8))
+
+    t_k, tS, tCp, tM, tB, tE, tT, tP, tQ, tPV, tEv, tot = {}, {}, {}, {}, {}, {}, {}, {}, {}, {}, {}, {}
     pvb = {s: (6 + s if s < 2 else s - 2) for s in range(NR)}
     nst = [0]
 
-    def load_v():
-        t_v.append(op("v", lambda e: e.quantize_mx(T.vc[:, 0:128], T.vs[:, 0:128], T.vin[:]), [("lv", 16)]))
+    def quant_k(b):
+        t_k[b] = op("v", lambda e: e.quantize_mx(T.kc[:, 256 * b:256 * b + 256], T.ks[:, 256 * b:256 * b + 256],
+                                                 T.kin[:, 1024 * b:1024 * b + 1024]), [("lk%d" % b, 16)])
+
+    def quant_one():
+        tot["V1"] = op("v", lambda e: e.quantize_mx(T.vc[:, 128:256], T.vs[:, 128:256], T.one[:]), [t_one])
+
+    def quant_v():
+        tot["V0"] = op("v", lambda e: e.quantize_mx(T.vc[:, 0:128], T.vs[:, 0:128], T.vin[:]), [("lv", 16)])
 
     def score(s):
-        deps = [t_q if s == 0 else ("q%d" % rk[s], 16)]
-        tS[s] = op("t", lambda e: e.matmul_mx(bank(s, 0, 512), T.qc[:, 128 * s:128 * s + 128], T.qs[:, 128 * s:128 * s + 128],
-                                              T.kc[:, 0:512], T.ks[:, 0:512], True, True), deps + t_k)
+        if s == 0:
+            tS[s] = [op("t", lambda e: e.matmul_mx(bank(6 * b, 0, 256), T.qc[:, 0:128], T.qs[:, 0:128], T.kc[:, 256 * b:256 * b + 256],
+                                                   T.ks[:, 256 * b:256 * b + 256], True, True), [t_q, t_k[b]]) for b in range(2)]
+        else:
+            tS[s] = [op("t", lambda e: e.matmul_mx(bank(s, 0, 512), T.qc[:, 128 * s:128 * s + 128], T.qs[:, 128 * s:128 * s + 128],
+                                                   T.kc[:, 0:512], T.ks[:, 0:512], True, True), [("q%d" % rk[s], 16), t_k[0], t_k[1]])]
 
     def half(s):
-        tCp[s] = op("s", lambda e: e.activation(T.s0[:, 256 * s:256 * s + 256], bank(s, 0, 256), AF.Copy), [tS[s]])
+        tCp[s] = op("s", lambda e: e.activation(T.s0[:, 256 * s:256 * s + 256], bank(s, 0, 256), AF.Copy), tS[s][:1])
 
     def maximum(s):
-        tM[s] = op("v", lambda e: e.tensor_tensor_scan(T.fm[:, 256 * s:256 * s + 256], T.s0[:, 256 * s:256 * s + 256], bank(s, 256, 512), LOW, mxm, mxm),
-                   [tCp[s], tS[s]])
+        other = bank(6, 0, 256) if s == 0 else bank(s, 256, 512)
+        tM[s] = op("v", lambda e: e.tensor_tensor_scan(T.fm[:, 256 * s:256 * s + 256], T.s0[:, 256 * s:256 * s + 256], other, LOW, mxm, mxm),
+                   [tCp[s]] + tS[s][-1:])
 
     def maximum_alone(s):
-        tM[s] = op("v", lambda e: e.tensor_reduce(T.fm[:, 256 * s + 255:256 * s + 256], bank(s, 0, 512), AxisListType.X, mxm), [tS[s]])
+        tM[s] = op("v", lambda e: e.tensor_reduce(T.fm[:, 256 * s + 255:256 * s + 256], bank(s, 0, 512), AxisListType.X, mxm), tS[s])
 
     def shift(s):
         m = T.fm[:, 256 * s + 255:256 * s + 256]
         tB[s] = op("s", lambda e: e.activation(T.nb[:, rk[s]:rk[s] + 1], m, AF.Copy, scale=-A), [tM[s], t_c])
 
     def own(s):
-        tCo[s] = op("s", lambda e: e.activation(T.cl[:, 4 * rank:4 * rank + 1], T.nb[:, rank:rank + 1], AF.Copy), [tB[s]])
+        tot["own"] = op("s", lambda e: e.activation(T.cl[:, 4 * rank:4 * rank + 1], T.nb[:, rank:rank + 1], AF.Copy), [tB[s]])
 
     def expo(s):
-        for b in range(4):
-            tE[s] = op("s", lambda e: e.activation(T.ee[:, 4 * s:4 * s + 4, 32 * b:32 * b + 32], T.ps[:, 512 * s + b:512 * s + 512:4], AF.Exp,
-                                                   bias=T.nb[:, rk[s]:rk[s] + 1], scale=A), [tB[s], tM[s]])
+        for k, lo, hi, w in [(0, 0, 2, 256), (6, 2, 4, 256)] if s == 0 else [(s, 0, 4, 512)]:
+            for b in range(4):
+                tE[s] = op("s", lambda e: e.activation(T.ee[:, 4 * s + lo:4 * s + hi, 32 * b:32 * b + 32], T.ps[:, 512 * k + b:512 * k + w:4],
+                                                       AF.Exp, bias=T.nb[:, rk[s]:rk[s] + 1], scale=A), [tB[s], tM[s]])
 
     def turn(s):
         c = 1024 * (s // 2)
         for b in range(4):
-            tT[s] = op("v", lambda e: e.transpose(T.zz[:, c + 4 * (s % 2) + b:c + 1024:8], T.ee[:, 4 * s + b, :]), [tE[s]])
+            out = T.zz[:, c + 4 * (s % 2) + b:c + 1024:8] if s < PAIRED else T.zz[:, 512 * s + b:512 * s + 512:4]
+            tT[s] = op("v", lambda e: e.transpose(out, T.ee[:, 4 * s + b, :]), [tE[s]])
 
     def moves(s):
-        for q in "ys" if s == 4 else "y":
-            need(q, [tT[s], tT[s + 1]])
+        pair = s < PAIRED
+        for q in "y" if pair else "ys":
+            need(q, [tT[s]] + ([tT[s + 1]] if pair else []))
         for a in range(4):
-            (g.scalar if s == 4 and a % 2 else g.sync).dma_start(T.yy[:, 64 * s + 32 * a:64 * s + 32 * a + 32, :],
-                                                                 T.zz[32 * a:32 * a + 32, 512 * s:512 * s + 1024]).then_inc(sem["y%d" % s], 16)
+            z, u = 512 * s, 512 * (s - PAIRED) + 128 * a
+            out = T.yy[:, 64 * s + 32 * a:64 * s + 32 * a + 32, :] if pair else T.y1[:, u:u + 128]
+            src = T.zz[32 * a:32 * a + 32, z:z + (1024 if pair else 512)]
+            (g.sync if pair or a % 2 == 0 else g.scalar).dma_start(out, src).then_inc(sem["y%d" % s], 16)
 
     def clamp(s):
-        c, h = 128 * (s // 2), 4 * (s % 2)
-        tP[s] = op("v", lambda e: e.tensor_scalar(T.pt[:, 512 * s:512 * s + 512], T.yy[:, c:c + 128, h:h + 4], FLOOR, None, mxm),
-                   [("y%d" % (s - s % 2), 64)])
+        c, h, u = 128 * (s // 2), 4 * (s % 2), 512 * (s - PAIRED)
+        src, y = (T.yy[:, c:c + 128, h:h + 4], s - s % 2) if s < PAIRED else (T.y1[:, u:u + 512], s)
+        tP[s] = op("v", lambda e: e.tensor_scalar(T.pt[:, 512 * s:512 * s + 512], src, FLOOR, None, mxm), [("y%d" % y, 64)])
 
     def quant(s):
         tQ[s] = op("v", lambda e: e.quantize_mx(T.pc[:, 128 * s:128 * s + 128], T.pp[:, 128 * s:128 * s + 128], T.pt[:, 512 * s:512 * s + 512]), [tP[s]])
 
     def values(s):
         tPV[s] = op("t", lambda e: e.matmul_mx(bank(pvb[s], 0, 256), T.pc[:, 128 * s:128 * s + 128], T.pp[:, 128 * s:128 * s + 128],
-                                               T.vc[:, 0:256], T.vs[:, 0:256], True, True), [tQ[s], t_v[0], t_V1] + ([tE[s - 2]] if s >= 2 else []))
+                                               T.vc[:, 0:256], T.vs[:, 0:256], True, True), [tQ[s], tot["V0"], tot["V1"], tE[s - 2 if s >= 2 else 0]])
 
     def evac(s):
         tEv[s] = op("s", lambda e: e.activation(T.sr[:, RW * s:RW * s + RN], bank(pvb[s], 0, RN), AF.Copy), [tPV[s]])
@@ -310,56 +327,95 @@ def rank_program(g, core, T, topo):
         else:
             send(src, [(b, T.ar[:, RW * rank:RW * rank + RN])], "a%d" % rank, width(core, b))
 
-    steps = dict(S=score, h=half, m=maximum, M=maximum_alone, b=shift, o=own, e=expo, t=turn, Y=moves, c=clamp, q=quant, x=values,
-                 v=evac, A=send_a)
-    for w in PLAN.split():
-        slots = [int(x) for x in w[1:]]
-        if w[0] == "V":
-            load_v()
-        elif w[0] == "C":
-            send_c(slots)
-        else:
-            for s in slots:
-                steps[w[0]](s)
+    def turn_c():
+        t = op("s", lambda e: e.activation(T.cc[:], T.nb[:], AF.Copy, scale=-1.0), [tB[s] for s in range(NR)])
+        tot["ct"] = op("v", lambda e: e.transpose(T.ct[:], T.cc[:]), [t])
 
-    t_cc = op("s", lambda e: e.activation(T.cc[:], T.nb[:], AF.Copy, scale=-1.0), [tB[s] for s in range(NR)])
-    t_ct = op("v", lambda e: e.transpose(T.ct[:], T.cc[:]), [t_cc])
-    for b in range(4):
-        store(T.c[:, 32 * b:32 * b + 32], T.ct[32 * b:32 * b + 6, :], [t_ct])
+    def store_c():
+        for b in range(4):
+            store(T.c[:, 32 * b:32 * b + 32], T.ct[32 * b:32 * b + NR, :], [tot["ct"]])
 
-    t_nm = op("v", lambda e: e.tensor_reduce(T.nm[:, 0:1], T.cl[:, 0:24:4], AxisListType.X, AluOpType.min), [("carr", 20), tCo[0]])
-    t_wt = op("s", lambda e: e.activation(T.wt[:, 0:6], T.cl[:, 0:24:4], AF.Exp, bias=T.nm[:, 0:1], scale=-1.0), [t_nm, t_w, ("carr", 20)])
-    t_wo = op("v", lambda e: e.transpose(T.wo[:], T.wt[:]), [t_wt])
-    for b in range(4):
-        store(T.w[:, 32 * b:32 * b + 32], T.wo[32 * b:32 * b + 6, :], [t_wo])
-    for s in range(NR):
+    def least():
+        tot["nm"] = op("v", lambda e: e.tensor_reduce(T.nm[:, 0:1], T.cl[:, 0:24:4], AxisListType.X, AluOpType.min), [("carr", 20), tot["own"]])
+
+    def weights():
+        tot["wt"] = op("s", lambda e: e.activation(T.wt[:, 0:6], T.cl[:, 0:24:4], AF.Exp, bias=T.nm[:, 0:1], scale=-1.0), [tot["nm"], t_w, ("carr", 20)])
+
+    def turn_w():
+        tot["wo"] = op("v", lambda e: e.transpose(T.wo[:], T.wt[:]), [tot["wt"]])
+
+    def store_w():
+        for b in range(4):
+            store(T.w[:, 32 * b:32 * b + 32], T.wo[32 * b:32 * b + NR, :], [tot["wo"]])
+
+    def store_p(s):
         store(T.p[rk[s]], T.pt[:, 512 * s:512 * s + 512], [tP[s]])
 
     def when(j):
         return DONE[order[j].index(core)] + HOP * ((j, core) in relay), j
 
-    acc = None
-    for k, j in enumerate([core] + sorted([j for j in cores if j != core], key=when)):
+    arrive = [core] + sorted([j for j in cores if j != core], key=when)
+
+    def came(k):
+        j = arrive[k]
         r = T.rank_of(j)
-        w, o = T.wt[:, r:r + 1], RW * r
-        here = [t_wt] + ([tEv[0]] if k == 0 else [("a%d" % r, width(relay.get((j, core), j), core))])
-        if k < NR - 1:
-            src = T.sr[:, 0:RN] if k == 0 else T.ar[:, o:o + RN]
-            out = T.ac[:, 0:RN] if k == 0 else T.uu[:, o:o + RN]
-            t = op("s", lambda e: e.activation(out, src, AF.Copy, scale=w), here)
-            acc = t if k == 0 else op("v", lambda e: e.tensor_tensor(T.ac[:, 0:RN], T.ac[:, 0:RN], T.uu[:, o:o + RN], add), [acc, t])
+        return T.wt[:, r:r + 1], RW * r, [tot["wt"]] + ([tPV[0]] if k == 0 else [("a%d" % r, width(relay.get((j, core), j), core))])
+
+    def weigh(k):
+        w, o, deps = came(k)
+        src, out = (bank(pvb[0], 0, RN), T.ac[:, 0:RN]) if k == 0 else (T.ar[:, o:o + RN], T.uu[:, o:o + RN])
+        tot["u%d" % k] = op("s", lambda e: e.activation(out, src, AF.Copy, scale=w), deps)
+        if k == 0:
+            tot["acc"] = tot["u0"]
+
+    def plus(k):
+        w, o, deps = came(k)
+        n = RN if k < NR - 2 else 128
+        tot["acc"] = tot["+%d" % k] = op("v", lambda e: e.tensor_tensor(T.ac[:, 0:n], T.ac[:, 0:n], T.uu[:, o:o + n], add), [tot["acc"], tot["u%d" % k]])
+
+    def rowsum(k):
+        w, o, deps = came(k)
+        old, new, t = (T.ac[:, 128:129], T.rc[:, 2:3], "+3") if k == NR - 2 else (T.rc[:, 2:3], T.rc[:, 1:2], "r4")
+        tot["r%d" % k] = op("s", lambda e: e.activation(new, T.ar[:, o + 128:o + 129], AF.Identity, bias=old, scale=w), deps + [tot[t]])
+
+    def final():
+        k = NR - 1
+        w, o, deps = came(k)
+        rowsum(k)
+        t_rc = op("v", lambda e: e.reciprocal(T.rc[:, 0:1], T.rc[:, 1:2]), [tot["r%d" % k]])
+        tu = op("s", lambda e: e.activation(T.uu[:, o:o + 128], T.ar[:, o:o + 128], AF.Copy, scale=w), deps)
+        ta, ton = {}, {}
+
+        def last_add(b):
+            h, x = 64 * (b // 2), b % 2
+            ta[b] = op("v", lambda e: e.tensor_tensor(T.ap[:, 32 * b:32 * b + 32], T.ac[:, h + x:h + 64:2], T.uu[:, o + h + x:o + h + 64:2], add),
+                       [tot["acc"], tu])
+
+        def divide(h):
+            ton[h] = op("v", lambda e: e.tensor_scalar(T.on[:, 64 * h:64 * h + 64], T.ap[:, 64 * h:64 * h + 64], T.rc[:, 0:1], None, mul),
+                        [t_rc, ta[2 * h + 1]])
+
+        def turn_o(h):
+            t = op("v", lambda e: e.transpose(T.ot[:, 64 * h:64 * h + 64], T.on[:, 64 * h:64 * h + 64]), [ton[h]])
+            for a in range(4):
+                store(T.o[64 * h:64 * h + 64, 32 * a:32 * a + 32], T.ot[32 * a:32 * a + 32, 64 * h:64 * h + 64], [t], "ys"[a % 2])
+
+        for f, x in ((last_add, 0), (last_add, 1), (last_add, 2), (divide, 0), (last_add, 3), (turn_o, 0), (divide, 1), (turn_o, 1)):
+            f(x)
+
+    steps = dict(k=quant_k, S=score, h=half, m=maximum, M=maximum_alone, b=shift, o=own, e=expo, t=turn, Y=moves, z=moves, c=clamp, q=quant,
+                 x=values, v=evac, A=send_a, P=store_p, u=weigh, r=rowsum)
+    steps["+"] = plus
+    plain = dict(I=quant_one, V=quant_v, J=turn_c, j=store_c, N=least, W=weights, O=turn_w, i=store_w, F=final)
+    for w in PLAN.split():
+        if w[0] in plain:
+            plain[w[0]]()
+        elif w[0] == "C":
+            send_c([int(x) for x in w[1:]])
         else:
-            t = op("s", lambda e: e.activation(T.rc[:, 1:2], T.ar[:, o + 128:o + 129], AF.Identity, bias=T.ac[:, 128:129], scale=w), here + [acc])
-            t_rc = op("v", lambda e: e.reciprocal(T.rc[:, 0:1], T.rc[:, 1:2]), [t])
-            tu = op("s", lambda e: e.activation(T.uu[:, o:o + 128], T.ar[:, o:o + 128], AF.Copy, scale=w), here)
-            ta = [op("v", lambda e: e.tensor_tensor(T.ap[:, 32 * b:32 * b + 32], T.ac[:, b:128:4], T.uu[:, o + b:o + 128:4], add), [acc, tu]) for b in range(4)]
-            ton = [op("v", lambda e: e.tensor_scalar(T.on[:, h:h + 64], T.ap[:, h:h + 64], T.rc[:, 0:1], None, mul), [t_rc, ta[h // 32 + 1]]) for h in (0, 64)]
-    tot = [op("v", lambda e: e.transpose(T.ot[:, h:h + 64], T.on[:, h:h + 64]), [ton[h // 64]]) for h in (0, 64)]
-    for a in range(4):
-        store(T.o[:, 32 * a:32 * a + 32], T.ot[32 * a:32 * a + 32, :], tot, "ys"[a % 2])
+            steps[w[0]](int(w[1:]))
 
     g.sync.wait_ge(sem["st"], nst[0])
-    for s in (0, 2, 4):
-        need("g", [("y%d" % s, 64)])
+    need("g", [("y%d" % s, 64) for s in (0, 2, 4, 5)])
     need("g", [(q, count[q]) for q in count])
     g.wait_ge(sem["sent"], sent[0])

import numpy as np
from concourse.bass import DstId, RemoteDMATransfer
from concourse.mybir import dt, AluOpType, AxisListType, ActivationFunctionType as AF

NR = 6
SIM = 80
A = float(np.float32(0.0125))
LOW = -1e29
FLOOR = float(np.exp(-20.0))
RW = 132
RN = 129

SCRATCH = {
    "qin": ("sbuf", [128, 512], "bfloat16"), "kin": ("sbuf", [128, 2048], "bfloat16"), "vin": ("sbuf", [128, 512], "bfloat16"),
    "zer": ("sbuf", [128, 512], "bfloat16"), "one": ("sbuf", [128, 512], "bfloat16"),
    "qc": ("sbuf", [128, 768], "float8_e4m3fn_x4"), "qs": ("sbuf", [128, 768], "uint8"),
    "kc": ("sbuf", [128, 512], "float8_e4m3fn_x4"), "ks": ("sbuf", [128, 512], "uint8"),
    "vc": ("sbuf", [128, 256], "float8_e4m3fn_x4"), "vs": ("sbuf", [128, 256], "uint8"),
    "pc": ("sbuf", [128, 768], "float8_e4m3fn_x4"), "pp": ("sbuf", [128, 768], "uint8"),
    "pt": ("sbuf", [128, 3072], "bfloat16"),
    "s0": ("sbuf", [128, 1536], "float32"), "fm": ("sbuf", [128, 1536], "float32"), "nb": ("sbuf", [128, 32], "float32"),
    "ee": ("sbuf", [128, 24, 128], "bfloat16"), "zz": ("sbuf", [128, 3072], "bfloat16"),
    "yy": ("sbuf", [128, 256, 8], "bfloat16"), "y1": ("sbuf", [128, 1024], "bfloat16"),
    "cc": ("sbuf", [128, 32], "float32"), "ct": ("sbuf", [128, 32], "float32"), "cl": ("sbuf", [128, 24], "float32"),
    "nm": ("sbuf", [128, 4], "float32"), "wt": ("sbuf", [128, 32], "float32"), "wo": ("sbuf", [128, 32], "float32"),
    "sr": ("sbuf", [128, NR * RW], "float32"), "ar": ("sbuf", [128, NR * RW], "float32"), "uu": ("sbuf", [128, NR * RW], "float32"),
    "ac": ("sbuf", [128, RW], "float32"), "ap": ("sbuf", [128, 128], "float32"), "rc": ("sbuf", [128, 4], "float32"),
    "on": ("sbuf", [128, 128], "float32"), "ot": ("sbuf", [128, 128], "float32"),
    "hc": ("sbuf", [128, 128], "float8_e4m3fn_x4"), "hs": ("sbuf", [128, 128], "uint8"),
    "hl": ("sbuf", [128, 8], "float32"), "ha": ("sbuf", [128, 2 * RW], "float32"),
    "ps": ("psum", [128, 4096], "float32"),
}
SEMAPHORES = (["v", "s", "t", "lq", "lv", "st", "sent", "carr", "hqc", "hqs", "hc0", "hc1", "ha0", "ha1", "y0", "y2", "y4", "y5", "lk0", "lk1"]
              + ["q%d" % i for i in range(NR)] + ["a%d" % i for i in range(NR)])

PAIRED = 4
DONE = (0, 0.4, 0.2, 0.7, 2.5, 3.1)
HOP = 0.5
PLAN = """k0 k1 S0 S1 h0 m0 I M1 b0 e0 S2 t0 b1 e1 S3 t1 h2 m2 M3 V o0 b2 e2 Y0 t2 b3 e3 t3 S4 h4 S5 m4 M5 c1 Y2 b4 e4 b5 e5 t4 q1 z4 t5 C1
c2 C23 q2 x1 z5 x2 v1 C45 A1 c3 q3 v2 P3 c4 x3 q4 x4 v3 A2 A3 v4 c5 q5 x5 A4 v5 c0 q0 J A5 x0 N W j P2 O i P5 u0 u1 u2 +1 u3 +2 u4 +3 r4
P0 P4 P1 +4 F"""


def engines(mask, n, k=0):
    bits = [e for e in range(16) if (mask >> e) & 1][k * n:k * n + n]
    return sum(1 << e for e in bits)


def links(topo, a, b):
    x, y, d = topo.chip(a), topo.chip(b), topo.die(a)
    if x == y:
        return []
    if topo.mates(x, y):
        return [("mate", d, x, y)]
    if topo.same_plane(x, y):
        return [("out", d, x), ("in", d, y)]
    m = [z for z in range(topo.chip(SIM - 1) + 1) if topo.mates(x, z)][0]
    return [("mate", d, x, m), ("out", d, m), ("in", d, y)]


def make_plan(T, topo):
    cores = list(T.cores)
    load = {}
    for a in cores:
        for b in cores:
            if a != b and topo.may_write(a, b):
                for l in links(topo, a, b):
                    load[l] = load.get(l, 0) + 1
    relay, used = {}, set(cores)
    for a in cores:
        barred = [b for b in cores if a != b and not topo.may_write(a, b)]
        for ch in sorted(set(topo.chip(b) for b in barred)):
            dsts = [b for b in barred if topo.chip(b) == ch]
            best = None
            for h in range(SIM):
                if h in used or not topo.may_write(a, h) or not all(topo.may_write(h, b) for b in dsts):
                    continue
                extra = {}
                for l in links(topo, a, h) + [l for b in dsts for l in links(topo, h, b)]:
                    extra[l] = extra.get(l, 0) + 1
                key = (max(load.get(l, 0) + n for l, n in extra.items()), sum(extra.values()), topo.die(h) != topo.die(a), h)
                if best is None or key < best[0]:
                    best = (key, h, extra)
            used.add(best[1])
            for l, n in best[2].items():
                load[l] = load.get(l, 0) + n
            for b in dsts:
                relay[(a, b)] = best[1]
    first = {}
    for (a, b), h in sorted(relay.items()):
        first[(a, h)] = min([y for (x, y), z in relay.items() if (x, z) == (a, h)], key=lambda y: ((y, a) not in relay, y))
    mate, early, late, sends, order = {}, {}, {}, {}, {}
    for j in cores:
        mate[j] = [i for i in cores if i != j and topo.chip(i) == topo.chip(j)]
        rest = [i for i in cores if i != j and i not in mate[j]]
        rest.sort(key=lambda i: ((i, j) in relay, (j, i) not in relay, i))
        early[j], late[j] = rest[:2], rest[2:]
    for j in cores:
        far = [b for b in cores if b != j and b not in mate[j]]
        rel = []
        for b in far:
            if (j, b) in relay and relay[(j, b)] not in rel:
                rel.append(relay[(j, b)])
        far = sorted([b for b in far if (j, b) not in relay], key=lambda b: (j not in early[b], (b, j) not in relay, b))
        sends[j] = mate[j] + rel[::-1] + far
    for j in cores:
        early[j].sort(key=lambda i: ((j, i) not in relay, [b for b in sends[i] if b in cores].index(j), i))
        late[j].sort(key=lambda i: ((i, j) not in relay, (i, j) in relay and first[(i, relay[(i, j)])] != j, -i))
        order[j] = [j] + mate[j] + early[j] + late[j]
    return relay, order, first, sends


def dest(topo, c):
    a = topo.addr(c)
    return DstId(rid=a[0], pnc=a[1])


def rank_program(g, core, T, topo):
    relay, order, first, sends = make_plan(T, topo)
    cores = list(T.cores)
    sem = T.sem
    sent = [0]

    def send(src, pieces, rsem, n, k=0):
        m = 0xFFFF
        for c, _ in pieces:
            m &= topo.mask(core, c)
        m = engines(m, n, k)
        g.remote_dma_fused([RemoteDMATransfer(dst_ids=[dest(topo, c) for c, _ in pieces], dma_engine_mask=m, remote_sem=sem[rsem],
                                              srcs=[src], dsts=[p for _, p in pieces])], local_sem=sem["sent"])
        sent[0] += n

    def width(a, b):
        return bin(topo.mask(a, b)).count("1")

    def codes(buf, a, b):
        return buf[:, a:b].bitcast(dt.uint8)

    def qslot(src, dst):
        return order[dst].index(src)

    def lane(b, n):
        return (n, 8 // n) if topo.chip(b) == topo.chip(core) else (n, 0)

    def put_q(src, dsts, cbuf, sbuf, name, n, k=0):
        to = {b: slice(128 * qslot(src, b), 128 * qslot(src, b) + 128) for b in dsts}
        send(codes(cbuf, 0, 128), [(b, codes(T.qc, to[b].start, to[b].stop)) for b in dsts], name, n, k)
        yield
        send(sbuf[:, 0:128], [(b, T.qs[:, to[b]]) for b in dsts], name, n, k)

    rank = T.rank_of(core)
    if rank is None:
        mine = sorted((a, b) for (a, b), h in relay.items() if h == core)
        if not mine:
            return
        src = mine[0][0]
        sr = T.rank_of(src)
        dsts = sorted([b for _, b in mine], key=lambda b: order[src].index(b))
        g.wait_ge(sem["hqc"], 8)
        for n, b in enumerate(sorted(dsts, key=lambda b: (b != first[(src, core)], b))):
            for _ in put_q(src, [b], T.hc, T.hs, "q%d" % sr, 8):
                if n == 0:
                    g.wait_ge(sem["hqs"], 8)
        for k, b in enumerate(dsts):
            g.wait_ge(sem["hc%d" % k], 4)
            send(T.hl[:, 4 * k:4 * k + 1], [(b, T.cl[:, 4 * sr:4 * sr + 1])], "carr", 4)
        for k, b in enumerate(dsts):
            g.wait_ge(sem["ha%d" % k], width(src, core))
            send(T.ha[:, RW * k:RW * k + RN], [(b, T.ar[:, RW * sr:RW * sr + RN])], "a%d" % sr, width(core, b))
        g.wait_ge(sem["sent"], sent[0])
        return

    me = order[core]
    rk = [T.rank_of(c) for c in me]
    queue = {"v": g.vector, "s": g.scalar, "t": g.tensor, "g": g, "y": g.sync}
    count = {"v": 0, "s": 0, "t": 0}
    seen = {q: {} for q in queue}

    def need(q, deps):
        want = {}
        for name, n in deps:
            want[name] = max(want.get(name, 0), n)
        for name, n in want.items():
            if seen[q].get(name, 0) < n:
                queue[q].wait_ge(sem[name], n)
                seen[q][name] = n

    def op(q, call, deps):
        need(q, deps)
        call(queue[q]).then_inc(sem[q], 1)
        count[q] += 1
        return (q, count[q])

    def bank(k, a, b):
        return T.ps[:, 512 * k + a:512 * k + b]

    add, mul, mxm = AluOpType.add, AluOpType.mult, AluOpType.max

    g.sync.dma_start(T.qin[:], T.q[:]).then_inc(sem["lq"], 16)
    for b in range(2):
        g.sync.dma_start(T.kin[:, 1024 * b:1024 * b + 1024], T.k[:, 1024 * b:1024 * b + 1024]).then_inc(sem["lk%d" % b], 16)
    need("y", [("lk1", 16)])
    g.sync.dma_start(T.vin[:], T.v[:]).then_inc(sem["lv"], 16)

    t_zer = op("v", lambda e: e.memset(T.zer[:], 0.0), [])
    t_one = op("s", lambda e: e.activation(T.one[:], T.zer[:], AF.Exp), [t_zer])
    t_w = op("v", lambda e: e.memset(T.wt[:], 0.0), [])
    t_c = op("v", lambda e: e.memset(T.nb[:], 0.0), [])

    t_q = op("v", lambda e: e.quantize_mx(T.qc[:, 0:128], T.qs[:, 0:128], T.qin[:]), [("lq", 16)])
    need("g", [t_q])
    for b in sends[core]:
        if b in cores:
            for _ in put_q(core, [b], T.qc, T.qs, "q%d" % rank, *lane(b, 8)):
                pass
        else:
            send(codes(T.qc, 0, 128), [(b, codes(T.hc, 0, 128))], "hqc", *lane(b, 8))
            send(T.qs[:, 0:128], [(b, T.hs[:, 0:128])], "hqs", *lane(b, 8))

    t_k, tS, tCp, tM, tB, tE, tT, tP, tQ, tPV, tEv, tot = {}, {}, {}, {}, {}, {}, {}, {}, {}, {}, {}, {}
    pvb = {s: (6 + s if s < 2 else s - 2) for s in range(NR)}
    nst = [0]

    def quant_k(b):
        t_k[b] = op("v", lambda e: e.quantize_mx(T.kc[:, 256 * b:256 * b + 256], T.ks[:, 256 * b:256 * b + 256],
                                                 T.kin[:, 1024 * b:1024 * b + 1024]), [("lk%d" % b, 16)])

    def quant_one():
        tot["V1"] = op("v", lambda e: e.quantize_mx(T.vc[:, 128:256], T.vs[:, 128:256], T.one[:]), [t_one])

    def quant_v():
        tot["V0"] = op("v", lambda e: e.quantize_mx(T.vc[:, 0:128], T.vs[:, 0:128], T.vin[:]), [("lv", 16)])

    def score(s):
        if s == 0:
            tS[s] = [op("t", lambda e: e.matmul_mx(bank(6 * b, 0, 256), T.qc[:, 0:128], T.qs[:, 0:128], T.kc[:, 256 * b:256 * b + 256],
                                                   T.ks[:, 256 * b:256 * b + 256], True, True), [t_q, t_k[b]]) for b in range(2)]
        else:
            tS[s] = [op("t", lambda e: e.matmul_mx(bank(s, 0, 512), T.qc[:, 128 * s:128 * s + 128], T.qs[:, 128 * s:128 * s + 128],
                                                   T.kc[:, 0:512], T.ks[:, 0:512], True, True), [("q%d" % rk[s], 16), t_k[0], t_k[1]])]

    def half(s):
        tCp[s] = op("s", lambda e: e.activation(T.s0[:, 256 * s:256 * s + 256], bank(s, 0, 256), AF.Copy), tS[s][:1])

    def maximum(s):
        other = bank(6, 0, 256) if s == 0 else bank(s, 256, 512)
        tM[s] = op("v", lambda e: e.tensor_tensor_scan(T.fm[:, 256 * s:256 * s + 256], T.s0[:, 256 * s:256 * s + 256], other, LOW, mxm, mxm),
                   [tCp[s]] + tS[s][-1:])

    def maximum_alone(s):
        tM[s] = op("v", lambda e: e.tensor_reduce(T.fm[:, 256 * s + 255:256 * s + 256], bank(s, 0, 512), AxisListType.X, mxm), tS[s])

    def shift(s):
        m = T.fm[:, 256 * s + 255:256 * s + 256]
        tB[s] = op("s", lambda e: e.activation(T.nb[:, rk[s]:rk[s] + 1], m, AF.Copy, scale=-A), [tM[s], t_c])

    def own(s):
        tot["own"] = op("s", lambda e: e.activation(T.cl[:, 4 * rank:4 * rank + 1], T.nb[:, rank:rank + 1], AF.Copy), [tB[s]])

    def expo(s):
        for k, lo, hi, w in [(0, 0, 2, 256), (6, 2, 4, 256)] if s == 0 else [(s, 0, 4, 512)]:
            for b in range(4):
                tE[s] = op("s", lambda e: e.activation(T.ee[:, 4 * s + lo:4 * s + hi, 32 * b:32 * b + 32], T.ps[:, 512 * k + b:512 * k + w:4],
                                                       AF.Exp, bias=T.nb[:, rk[s]:rk[s] + 1], scale=A), [tB[s], tM[s]])

    def turn(s):
        c = 1024 * (s // 2)
        for b in range(4):
            out = T.zz[:, c + 4 * (s % 2) + b:c + 1024:8] if s < PAIRED else T.zz[:, 512 * s + b:512 * s + 512:4]
            tT[s] = op("v", lambda e: e.transpose(out, T.ee[:, 4 * s + b, :]), [tE[s]])

    def moves(s):
        pair = s < PAIRED
        for q in "y" if pair else "ys":
            need(q, [tT[s]] + ([tT[s + 1]] if pair else []))
        for a in range(4):
            z, u = 512 * s, 512 * (s - PAIRED) + 128 * a
            out = T.yy[:, 64 * s + 32 * a:64 * s + 32 * a + 32, :] if pair else T.y1[:, u:u + 128]
            src = T.zz[32 * a:32 * a + 32, z:z + (1024 if pair else 512)]
            (g.sync if pair or a % 2 == 0 else g.scalar).dma_start(out, src).then_inc(sem["y%d" % s], 16)

    def clamp(s):
        c, h, u = 128 * (s // 2), 4 * (s % 2), 512 * (s - PAIRED)
        src, y = (T.yy[:, c:c + 128, h:h + 4], s - s % 2) if s < PAIRED else (T.y1[:, u:u + 512], s)
        tP[s] = op("v", lambda e: e.tensor_scalar(T.pt[:, 512 * s:512 * s + 512], src, FLOOR, None, mxm), [("y%d" % y, 64)])

    def quant(s):
        tQ[s] = op("v", lambda e: e.quantize_mx(T.pc[:, 128 * s:128 * s + 128], T.pp[:, 128 * s:128 * s + 128], T.pt[:, 512 * s:512 * s + 512]), [tP[s]])

    def values(s):
        tPV[s] = op("t", lambda e: e.matmul_mx(bank(pvb[s], 0, 256), T.pc[:, 128 * s:128 * s + 128], T.pp[:, 128 * s:128 * s + 128],
                                               T.vc[:, 0:256], T.vs[:, 0:256], True, True), [tQ[s], tot["V0"], tot["V1"], tE[s - 2 if s >= 2 else 0]])

    def evac(s):
        tEv[s] = op("s", lambda e: e.activation(T.sr[:, RW * s:RW * s + RN], bank(pvb[s], 0, RN), AF.Copy), [tPV[s]])

    def store(out, in_, deps, q="y"):
        need(q, deps)
        (g.sync if q == "y" else g.scalar).dma_start(out, in_).then_inc(sem["st"], 16)
        nst[0] += 16

    def hk(b):
        h = relay[(core, b)]
        return h, [x for x in me if relay.get((core, x)) == h].index(b)

    def send_c(slots):
        need("g", [tB[s] for s in slots])
        trs, on = [], {}
        for s in slots:
            b, to, land, name = me[s], me[s], T.cl[:, 4 * rank:4 * rank + 1], "carr"
            if (core, b) in relay:
                to, k = hk(b)
                land, name = T.hl[:, 4 * k:4 * k + 1], "hc%d" % k
            n, k = lane(to, 4)
            on[k] = on.get(k, -1) + 1
            trs.append(RemoteDMATransfer(dst_ids=[dest(topo, to)], dma_engine_mask=engines(topo.mask(core, to), n, k + on[k]), remote_sem=sem[name],
                                         srcs=[T.nb[:, rk[s]:rk[s] + 1]], dsts=[land]))
            sent[0] += n
        g.remote_dma_fused(trs, local_sem=sem["sent"])

    def send_a(s):
        b, src = me[s], T.sr[:, RW * s:RW * s + RN]
        need("g", [tEv[s]])
        if (core, b) in relay:
            h, k = hk(b)
            send(src, [(h, T.ha[:, RW * k:RW * k + RN])], "ha%d" % k, width(core, h))
        else:
            send(src, [(b, T.ar[:, RW * rank:RW * rank + RN])], "a%d" % rank, width(core, b))

    def turn_c():
        t = op("s", lambda e: e.activation(T.cc[:], T.nb[:], AF.Copy, scale=-1.0), [tB[s] for s in range(NR)])
        tot["ct"] = op("v", lambda e: e.transpose(T.ct[:], T.cc[:]), [t])

    def store_c():
        for b in range(4):
            store(T.c[:, 32 * b:32 * b + 32], T.ct[32 * b:32 * b + NR, :], [tot["ct"]])

    def least():
        tot["nm"] = op("v", lambda e: e.tensor_reduce(T.nm[:, 0:1], T.cl[:, 0:24:4], AxisListType.X, AluOpType.min), [("carr", 20), tot["own"]])

    def weights():
        tot["wt"] = op("s", lambda e: e.activation(T.wt[:, 0:6], T.cl[:, 0:24:4], AF.Exp, bias=T.nm[:, 0:1], scale=-1.0), [tot["nm"], t_w, ("carr", 20)])

    def turn_w():
        tot["wo"] = op("v", lambda e: e.transpose(T.wo[:], T.wt[:]), [tot["wt"]])

    def store_w():
        for b in range(4):
            store(T.w[:, 32 * b:32 * b + 32], T.wo[32 * b:32 * b + NR, :], [tot["wo"]])

    def store_p(s):
        store(T.p[rk[s]], T.pt[:, 512 * s:512 * s + 512], [tP[s]])

    def when(j):
        return DONE[order[j].index(core)] + HOP * ((j, core) in relay), j

    arrive = [core] + sorted([j for j in cores if j != core], key=when)

    def came(k):
        j = arrive[k]
        r = T.rank_of(j)
        return T.wt[:, r:r + 1], RW * r, [tot["wt"]] + ([tPV[0]] if k == 0 else [("a%d" % r, width(relay.get((j, core), j), core))])

    def weigh(k):
        w, o, deps = came(k)
        src, out = (bank(pvb[0], 0, RN), T.ac[:, 0:RN]) if k == 0 else (T.ar[:, o:o + RN], T.uu[:, o:o + RN])
        tot["u%d" % k] = op("s", lambda e: e.activation(out, src, AF.Copy, scale=w), deps)
        if k == 0:
            tot["acc"] = tot["u0"]

    def plus(k):
        w, o, deps = came(k)
        n = RN if k < NR - 2 else 128
        tot["acc"] = tot["+%d" % k] = op("v", lambda e: e.tensor_tensor(T.ac[:, 0:n], T.ac[:, 0:n], T.uu[:, o:o + n], add), [tot["acc"], tot["u%d" % k]])

    def rowsum(k):
        w, o, deps = came(k)
        old, new, t = (T.ac[:, 128:129], T.rc[:, 2:3], "+3") if k == NR - 2 else (T.rc[:, 2:3], T.rc[:, 1:2], "r4")
        tot["r%d" % k] = op("s", lambda e: e.activation(new, T.ar[:, o + 128:o + 129], AF.Identity, bias=old, scale=w), deps + [tot[t]])

    def final():
        k = NR - 1
        w, o, deps = came(k)
        rowsum(k)
        t_rc = op("v", lambda e: e.reciprocal(T.rc[:, 0:1], T.rc[:, 1:2]), [tot["r%d" % k]])
        tu = op("s", lambda e: e.activation(T.uu[:, o:o + 128], T.ar[:, o:o + 128], AF.Copy, scale=w), deps)
        ta, ton = {}, {}

        def last_add(b):
            h, x = 64 * (b // 2), b % 2
            ta[b] = op("v", lambda e: e.tensor_tensor(T.ap[:, 32 * b:32 * b + 32], T.ac[:, h + x:h + 64:2], T.uu[:, o + h + x:o + h + 64:2], add),
                       [tot["acc"], tu])

        def divide(h):
            ton[h] = op("v", lambda e: e.tensor_scalar(T.on[:, 64 * h:64 * h + 64], T.ap[:, 64 * h:64 * h + 64], T.rc[:, 0:1], None, mul),
                        [t_rc, ta[2 * h + 1]])

        def turn_o(h):
            t = op("v", lambda e: e.transpose(T.ot[:, 64 * h:64 * h + 64], T.on[:, 64 * h:64 * h + 64]), [ton[h]])
            for a in range(4):
                store(T.o[64 * h:64 * h + 64, 32 * a:32 * a + 32], T.ot[32 * a:32 * a + 32, 64 * h:64 * h + 64], [t], "ys"[a % 2])

        for f, x in ((last_add, 0), (last_add, 1), (last_add, 2), (divide, 0), (last_add, 3), (turn_o, 0), (divide, 1), (turn_o, 1)):
            f(x)

    steps = dict(k=quant_k, S=score, h=half, m=maximum, M=maximum_alone, b=shift, o=own, e=expo, t=turn, Y=moves, z=moves, c=clamp, q=quant,
                 x=values, v=evac, A=send_a, P=store_p, u=weigh, r=rowsum)
    steps["+"] = plus
    plain = dict(I=quant_one, V=quant_v, J=turn_c, j=store_c, N=least, W=weights, O=turn_w, i=store_w, F=final)
    for w in PLAN.split():
        if w[0] in plain:
            plain[w[0]]()
        elif w[0] == "C":
            send_c([int(x) for x in w[1:]])
        else:
            steps[w[0]](int(w[1:]))

    g.sync.wait_ge(sem["st"], nst[0])
    need("g", [("y%d" % s, 64) for s in (0, 2, 4, 5)])
    need("g", [(q, count[q]) for q in count])
    g.wait_ge(sem["sent"], sent[0])
